import numpy as np
import ml_dtypes


def mxq(x, axis, fmt="e4m3"):
    dtype, down = {"e4m3": (ml_dtypes.float8_e4m3fn, 7), "e5m2": (ml_dtypes.float8_e5m2, 14)}[fmt]
    v = np.moveaxis(np.asarray(x, np.float32).astype(ml_dtypes.bfloat16).astype(np.float64), axis, -1)
    blocks = v.reshape(v.shape[:-1] + (-1, 32))
    amax = np.abs(blocks).max(-1, keepdims=True)
    byte = np.maximum(np.where(amax > 0, np.frexp(amax)[1] - 1 + 127, 0) - down, 1)
    scale = np.exp2(byte - 127.0)
    codes = (blocks / scale).astype(np.float32).astype(dtype).astype(np.float64)
    return np.moveaxis((codes * scale).reshape(v.shape), -1, axis)


WIDE = False


def mx_kscale(k):
    if not WIDE:
        return np.ones(k)
    levels = np.array([10, -10, 5, -5, 0])
    if k % 512:
        return np.exp2(np.random.permutation(np.resize(levels, k // 32))).repeat(32)
    a = np.empty((k // 512, 16))
    for p in range(k // 512):
        a[p, :8] = np.random.permutation(np.resize(levels, 8))
        for g in range(8):
            far = levels[np.abs(levels - a[p, g]) >= 10]
            a[p, g + 8] = far[np.random.randint(len(far))]
    return np.exp2(a.ravel()).repeat(32)


def f64(x):
    return np.asarray(x).astype(np.float64)


def striped8(idx):
    return np.concatenate([x.reshape(-1, 16).T for x in idx]).astype(np.uint16)


def runs(offs, k):
    lists = np.stack([offs[16 * r : 16 * r + 16].T.reshape(-1) for r in range(8)]).astype(np.int64)
    return lists[np.arange(k) % 512 // 64]


def pack_weight(w):
    k, n = w.shape
    w = f64(np.asarray(w, np.float32).astype(ml_dtypes.bfloat16)).reshape(k // 32, 32, n)
    amax = np.abs(w).max(1)
    byte = np.clip(np.where(amax > 0, np.frexp(amax)[1] - 1 + 127 - 7, 1), 1, 254)
    scaled = (w * np.exp2(127.0 - byte)[:, None, :]).reshape(k, n).astype(np.float32)
    words = np.ascontiguousarray(scaled.reshape(k // 512, 128, 4, n).transpose(0, 1, 3, 2)).astype(ml_dtypes.float8_e4m3fn).view(np.uint8)
    return words, np.ascontiguousarray(byte.astype(np.uint8).reshape(k // 512, 16, n))


def unpack_weight(words, scales):
    g, p, n, _ = words.shape
    vals = np.ascontiguousarray(words).view(ml_dtypes.float8_e4m3fn).astype(np.float64) * np.repeat(np.exp2(scales.astype(np.float64) - 127.0), 8, axis=1)[..., None]
    return vals.transpose(0, 1, 3, 2).reshape(g * 512, n)


def gelu(v):
    return 0.5 * v * (1.0 + np.tanh(np.sqrt(2.0 / np.pi) * (v + 0.044715 * v**3)))


K, T, S, H, N = 512, 2048, 512, 512, 128


def setup_inputs():
    n = np.random.standard_normal
    s = mx_kscale(K)[:, None]
    u = mx_kscale(H)
    packed_xT = pack_weight(n((K, T)) * s)
    return {
        "x_words": packed_xT[0],
        "x_scales": packed_xT[1],
        "w1": (n((K, N)) / np.sqrt(2 * K) / s).astype(np.float32),
        "w2": (n((K, H)) / np.sqrt(K) / s * u).astype(np.float32),
        "w3": (n((H, N)) / np.sqrt(2 * H) / u[:, None]).astype(np.float32),
        "offs": striped8(np.stack([np.random.permutation(T)[:S] for _ in range(8)])),
    }


def reference(x_words, x_scales, w1, w2, w3, offs):
    xq = unpack_weight(x_words, x_scales)[np.arange(K)[:, None], runs(offs, K)]
    h = gelu(mxq(f64(w2), 0, "e4m3").T @ xq)
    return mxq(f64(w1), 0, "e4m3").T @ xq + mxq(f64(w3), 0, "e4m3").T @ mxq(h, 0, "e4m3")

@@ -1,0 +1,115 @@
+from contextlib import ExitStack
+
+import concourse.mybir as mybir
+
+K, T, S, H, N = 512, 2048, 512, 512, 128
+FLOPS = 2 * S * (K * H + K * N + H * N)
+
+F32 = mybir.dt.float32
+BF16 = mybir.dt.bfloat16
+I32 = mybir.dt.int32
+U32 = mybir.dt.uint32
+U16 = mybir.dt.uint16
+U8 = mybir.dt.uint8
+FP8X4 = mybir.dt.float8_e4m3fn_x4
+GELU = mybir.ActivationFunctionType.Gelu_apprx_tanh
+
+P = 128
+PACK = 4
+GATHER = 256
+CHUNK = 128
+W2_SCALAR = 40
+
+
+def tile_picked_phlora_gelu_p_kernel(tc, x_words, x_scales, w1, w2, w3, offs, out):
+    nc = tc.nc
+    with ExitStack() as ctx:
+        keep = ctx.enter_context(tc.tile_pool(name="keep", bufs=1))
+        psum = ctx.enter_context(tc.psum_pool(name="psum", bufs=1))
+
+        lists = keep.tile([P, S // 16], U16, name="lists")
+        nc.sync.dma_start(lists[:], offs)
+
+        w2_raw = keep.tile([P, PACK, H], F32, name="w2_raw")
+        nc.sync.dma_start(w2_raw[:], w2.rearrange("(p j) c -> p j c", j=PACK))
+        word_table = keep.tile([P, T], U32, name="word_table", align_bytes=64)
+        nc.sync.dma_start(word_table[:].bitcast(I32), x_words[0].rearrange("p n t -> p (n t)").bitcast(I32))
+        w1_raw = keep.tile([P, PACK, N], F32, name="w1_raw")
+        nc.sync.dma_start(w1_raw[:], w1.rearrange("(p j) c -> p j c", j=PACK))
+        w3_raw = keep.tile([P, PACK, N], F32, name="w3_raw")
+        nc.sync.dma_start(w3_raw[:], w3.rearrange("(p j) c -> p j c", j=PACK))
+
+        scale_table = keep.tile([P, T], U8, name="scale_table", align_bytes=64)
+        nc.vector.memset(scale_table[:].bitcast(I32), 0)
+        scale_rows = x_scales[0].rearrange("(r e) c -> e r c", e=2)
+        for e in range(2):
+            nc.scalar.dma_start(scale_table[e:P:16, :].bitcast(I32), scale_rows[e].bitcast(I32))
+
+        warm_in = keep.tile([P, 1], F32, name="warm_in")
+        warm_out = keep.tile([P, 1], F32, name="warm_out")
+        nc.vector.memset(warm_in[:], 0.0)
+        nc.scalar.activation(warm_out[:], warm_in[:], GELU)
+
+        picked_scales = keep.tile([P, S], U8, name="picked_scales", align_bytes=64)
+        nc.vector.tensor_copy(picked_scales[:], scale_table[:].indirect(lists[:]))
+        x_plane = keep.tile([P, S], U8, name="x_plane", align_bytes=64)
+        nc.vector.tensor_copy(x_plane[:].bitcast(I32), picked_scales[:].bitcast(I32))
+        for e in range(2):
+            nc.scalar.dma_start(x_plane[2 + e : P : 32, :].bitcast(I32), picked_scales[16 + e : P : 32, :].bitcast(I32))
+
+        w2_bf = keep.tile([P, PACK, P, PACK], BF16, name="w2_bf", align_bytes=64)
+        w2_dst = w2_bf[:].rearrange("p t m j -> p m t j")
+        w2_src = w2_raw[:].rearrange("p j (m t) -> p m t j", t=PACK)
+        nc.scalar.copy(w2_dst[:, :W2_SCALAR], w2_src[:, :W2_SCALAR])
+        nc.vector.tensor_copy(w2_dst[:, W2_SCALAR:], w2_src[:, W2_SCALAR:])
+        w2_codes = keep.tile([P, H], U32, name="w2_codes", align_bytes=64)
+        w2_plane = keep.tile([P, H], U8, name="w2_plane", align_bytes=64)
+        nc.vector.quantize_mx(out=w2_codes[:].bitcast(FP8X4), scales=w2_plane[:], in_=w2_bf[:].rearrange("p t m j -> p (t m j)"))
+
+        x_codes = []
+        for g in range(S // GATHER):
+            picked = keep.tile([P, GATHER], U32, name="x_codes%d" % g, align_bytes=64)
+            cols = GATHER // 16
+            nc.vector.tensor_copy(picked[:], word_table[:].indirect(lists[:, g * cols : (g + 1) * cols]))
+            x_codes.append(picked)
+
+        def x_operand(c):
+            g, lo = divmod(c * CHUNK, GATHER)
+            return x_codes[g][:, lo : lo + CHUNK].bitcast(FP8X4), x_plane[:, c * CHUNK : (c + 1) * CHUNK]
+
+        chunks = S // CHUNK
+        hidden = []
+        for c in range(chunks):
+            bank = psum.tile([P, PACK, CHUNK], F32, name="hidden%d" % c)
+            codes, plane = x_operand(c)
+            for t in range(PACK):
+                cols = slice(t * P, (t + 1) * P)
+                nc.tensor.matmul_mx(out=bank[:, t, :], lhsT=w2_codes[:, cols].bitcast(FP8X4), lhsT_scale=w2_plane[:, cols],
+                                    rhs=codes, rhs_scale=plane, start=True, stop=True)
+            hidden.append(bank)
+
+        w13_bf = keep.tile([P, 2, N, PACK], BF16, name="w13_bf", align_bytes=64)
+        nc.scalar.copy(w13_bf[:, 0].rearrange("p (c i) j -> p c j i", i=4), w1_raw[:].rearrange("p j (c i) -> p c j i", i=4))
+        nc.vector.tensor_copy(w13_bf[:, 1].rearrange("p (c i) j -> p c j i", i=4), w3_raw[:].rearrange("p j (c i) -> p c j i", i=4))
+        w13_codes = keep.tile([P, 2 * N], U32, name="w13_codes", align_bytes=64)
+        w13_plane = keep.tile([P, 2 * N], U8, name="w13_plane", align_bytes=64)
+        nc.vector.quantize_mx(out=w13_codes[:].bitcast(FP8X4), scales=w13_plane[:], in_=w13_bf[:].rearrange("p w c j -> p (w c j)"))
+
+        for c in range(chunks):
+            h_bf = keep.tile([P, CHUNK, PACK], BF16, name="h_bf%d" % c, align_bytes=64)
+            nc.scalar.activation(h_bf[:], hidden[c][:].rearrange("p t n -> p n t"), GELU)
+            h_codes = keep.tile([P, CHUNK], U32, name="h_codes%d" % c, align_bytes=64)
+            h_plane = keep.tile([P, CHUNK], U8, name="h_plane%d" % c, align_bytes=64)
+            nc.vector.quantize_mx(out=h_codes[:].bitcast(FP8X4), scales=h_plane[:], in_=h_bf[:].rearrange("p n t -> p (n t)"))
+            acc = psum.tile([P, CHUNK], F32, name="acc%d" % c)
+            codes, plane = x_operand(c)
+            nc.tensor.matmul_mx(out=acc[:], lhsT=w13_codes[:, :N].bitcast(FP8X4), lhsT_scale=w13_plane[:, :N],
+                                rhs=codes, rhs_scale=plane, start=True, stop=False)
+            nc.tensor.matmul_mx(out=acc[:], lhsT=w13_codes[:, N:].bitcast(FP8X4), lhsT_scale=w13_plane[:, N:],
+                                rhs=h_codes[:].bitcast(FP8X4), rhs_scale=h_plane[:], start=False, stop=True)
+            result = keep.tile([P, CHUNK], F32, name="result%d" % c)
+            if c == chunks - 2:
+                nc.scalar.copy(result[:], acc[:])
+            else:
+                nc.vector.tensor_copy(result[:], acc[:])
+            nc.sync.dma_start(out[:, c * CHUNK : (c + 1) * CHUNK], result[:])

@@ -27,23 +27,21 @@ def tile_picked_phlora_gelu_p_kernel(tc, x_words, x_scales, w1, w2, w3, offs, ou
         keep = ctx.enter_context(tc.tile_pool(name="keep", bufs=1))
         psum = ctx.enter_context(tc.psum_pool(name="psum", bufs=1))
 
-        lists = keep.tile([P, S // 16], U16, name="lists")
-        nc.sync.dma_start(lists[:], offs)
+        scale_table = keep.tile([P, T], U8, name="scale_table", tag="early_late", align_bytes=64)
+        nc.vector.memset(scale_table[:].bitcast(I32), 0)
 
         w2_raw = keep.tile([P, PACK, H], F32, name="w2_raw")
-        nc.sync.dma_start(w2_raw[:], w2.rearrange("(p j) c -> p j c", j=PACK))
+        w2_rows = w2.rearrange("(p j) c -> p j c", j=PACK)
+        nc.sync.dma_start(w2_raw[:, :1], w2_rows[:, :1])
+        lists = keep.tile([P, S // 16], U16, name="lists")
+        nc.sync.dma_start(lists[:], offs)
+        nc.sync.dma_start(scale_table[0:P:8, :].bitcast(I32), x_scales[0].bitcast(I32))
+        nc.sync.dma_start(w2_raw[:, 1:], w2_rows[:, 1:])
         word_table = keep.tile([P, T], U32, name="word_table", align_bytes=64)
         nc.sync.dma_start(word_table[:].bitcast(I32), x_words[0].rearrange("p n t -> p (n t)").bitcast(I32))
-        w1_raw = keep.tile([P, PACK, N], F32, name="w1_raw")
-        nc.sync.dma_start(w1_raw[:], w1.rearrange("(p j) c -> p j c", j=PACK))
-        w3_raw = keep.tile([P, PACK, N], F32, name="w3_raw")
-        nc.sync.dma_start(w3_raw[:], w3.rearrange("(p j) c -> p j c", j=PACK))
 
-        scale_table = keep.tile([P, T], U8, name="scale_table", align_bytes=64)
-        nc.vector.memset(scale_table[:].bitcast(I32), 0)
-        scale_rows = x_scales[0].rearrange("(r e) c -> e r c", e=2)
-        for e in range(2):
-            nc.scalar.dma_start(scale_table[e:P:16, :].bitcast(I32), scale_rows[e].bitcast(I32))
+        x_plane = keep.tile([P, S], U8, name="x_plane", align_bytes=64)
+        nc.vector.memset(x_plane[:].bitcast(I32), 0)
 
         warm_in = keep.tile([P, 1], F32, name="warm_in")
         warm_out = keep.tile([P, 1], F32, name="warm_out")
@@ -52,10 +50,12 @@ def tile_picked_phlora_gelu_p_kernel(tc, x_words, x_scales, w1, w2, w3, offs, ou
 
         picked_scales = keep.tile([P, S], U8, name="picked_scales", align_bytes=64)
         nc.vector.tensor_copy(picked_scales[:], scale_table[:].indirect(lists[:]))
-        x_plane = keep.tile([P, S], U8, name="x_plane", align_bytes=64)
-        nc.vector.tensor_copy(x_plane[:].bitcast(I32), picked_scales[:].bitcast(I32))
-        for e in range(2):
-            nc.scalar.dma_start(x_plane[2 + e : P : 32, :].bitcast(I32), picked_scales[16 + e : P : 32, :].bitcast(I32))
+        for r in range(4):
+            nc.sync.dma_start(x_plane[r:P:32, :].bitcast(I32), picked_scales[8 * r : P : 32, :].bitcast(I32))
+
+        w13_raw = keep.tile([P, 2, PACK, N], F32, name="w13_raw", tag="early_late", align_bytes=64)
+        nc.sync.dma_start(w13_raw[:, 0], w1.rearrange("(p j) c -> p j c", j=PACK))
+        nc.sync.dma_start(w13_raw[:, 1], w3.rearrange("(p j) c -> p j c", j=PACK))
 
         w2_bf = keep.tile([P, PACK, P, PACK], BF16, name="w2_bf", align_bytes=64)
         w2_dst = w2_bf[:].rearrange("p t m j -> p m t j")
@@ -89,8 +89,7 @@ def tile_picked_phlora_gelu_p_kernel(tc, x_words, x_scales, w1, w2, w3, offs, ou
             hidden.append(bank)
 
         w13_bf = keep.tile([P, 2, N, PACK], BF16, name="w13_bf", align_bytes=64)
-        nc.scalar.copy(w13_bf[:, 0].rearrange("p (c i) j -> p c j i", i=4), w1_raw[:].rearrange("p j (c i) -> p c j i", i=4))
-        nc.vector.tensor_copy(w13_bf[:, 1].rearrange("p (c i) j -> p c j i", i=4), w3_raw[:].rearrange("p j (c i) -> p c j i", i=4))
+        nc.vector.tensor_copy(w13_bf[:].rearrange("p w (c i) j -> p w c j i", i=4), w13_raw[:].rearrange("p w j (c i) -> p w c j i", i=4))
         w13_codes = keep.tile([P, 2 * N], U32, name="w13_codes", align_bytes=64)
         w13_plane = keep.tile([P, 2 * N], U8, name="w13_plane", align_bytes=64)
         nc.vector.quantize_mx(out=w13_codes[:].bitcast(FP8X4), scales=w13_plane[:], in_=w13_bf[:].rearrange("p w c j -> p (w c j)"))

@@ -18,7 +18,9 @@ P = 128
 PACK = 4
 GATHER = 256
 CHUNK = 128
-W2_SCALAR = 40
+W2_SCALAR = 48
+W2_FIRST = 768
+OUT_PIECES = ((0, 256), (256, 384), (384, 512))
 
 
 def tile_picked_phlora_gelu_p_kernel(tc, x_words, x_scales, w1, w2, w3, offs, out):
@@ -30,13 +32,13 @@ def tile_picked_phlora_gelu_p_kernel(tc, x_words, x_scales, w1, w2, w3, offs, ou
         scale_table = keep.tile([P, T], U8, name="scale_table", tag="early_late", align_bytes=64)
         nc.vector.memset(scale_table[:].bitcast(I32), 0)
 
-        w2_raw = keep.tile([P, PACK, H], F32, name="w2_raw")
-        w2_rows = w2.rearrange("(p j) c -> p j c", j=PACK)
-        nc.sync.dma_start(w2_raw[:, :1], w2_rows[:, :1])
+        w2_raw = keep.tile([P, PACK * H], F32, name="w2_raw")
+        w2_rows = w2.rearrange("(p j) c -> p (j c)", j=PACK)
+        nc.sync.dma_start(w2_raw[:, :W2_FIRST], w2_rows[:, :W2_FIRST])
         lists = keep.tile([P, S // 16], U16, name="lists")
         nc.sync.dma_start(lists[:], offs)
         nc.sync.dma_start(scale_table[0:P:8, :].bitcast(I32), x_scales[0].bitcast(I32))
-        nc.sync.dma_start(w2_raw[:, 1:], w2_rows[:, 1:])
+        nc.sync.dma_start(w2_raw[:, W2_FIRST:], w2_rows[:, W2_FIRST:])
         word_table = keep.tile([P, T], U32, name="word_table", align_bytes=64)
         nc.sync.dma_start(word_table[:].bitcast(I32), x_words[0].rearrange("p n t -> p (n t)").bitcast(I32))
 
@@ -59,7 +61,7 @@ def tile_picked_phlora_gelu_p_kernel(tc, x_words, x_scales, w1, w2, w3, offs, ou
 
         w2_bf = keep.tile([P, PACK, P, PACK], BF16, name="w2_bf", align_bytes=64)
         w2_dst = w2_bf[:].rearrange("p t m j -> p m t j")
-        w2_src = w2_raw[:].rearrange("p j (m t) -> p m t j", t=PACK)
+        w2_src = w2_raw[:].rearrange("p (j m t) -> p m t j", j=PACK, t=PACK)
         nc.scalar.copy(w2_dst[:, :W2_SCALAR], w2_src[:, :W2_SCALAR])
         nc.vector.tensor_copy(w2_dst[:, W2_SCALAR:], w2_src[:, W2_SCALAR:])
         w2_codes = keep.tile([P, H], U32, name="w2_codes", align_bytes=64)
@@ -88,27 +90,32 @@ def tile_picked_phlora_gelu_p_kernel(tc, x_words, x_scales, w1, w2, w3, offs, ou
                                     rhs=codes, rhs_scale=plane, start=True, stop=True)
             hidden.append(bank)
 
-        w13_bf = keep.tile([P, 2, N, PACK], BF16, name="w13_bf", align_bytes=64)
-        nc.vector.tensor_copy(w13_bf[:].rearrange("p w (c i) j -> p w c j i", i=4), w13_raw[:].rearrange("p w j (c i) -> p w c j i", i=4))
-        w13_codes = keep.tile([P, 2 * N], U32, name="w13_codes", align_bytes=64)
-        w13_plane = keep.tile([P, 2 * N], U8, name="w13_plane", align_bytes=64)
-        nc.vector.quantize_mx(out=w13_codes[:].bitcast(FP8X4), scales=w13_plane[:], in_=w13_bf[:].rearrange("p w c j -> p (w c j)"))
+        w13_bf = keep.tile([P, 2, N, PACK], BF16, name="w13_bf", tag="w13_then_h", align_bytes=64)
+        w13_codes = keep.tile([P, 2, N], U32, name="w13_codes", align_bytes=64)
+        w13_plane = keep.tile([P, 2, N], U8, name="w13_plane", align_bytes=64)
+        for w in range(2):
+            nc.vector.tensor_copy(w13_bf[:, w].rearrange("p (c i) j -> p c j i", i=4), w13_raw[:, w].rearrange("p j (c i) -> p c j i", i=4))
+        for w in range(2):
+            nc.vector.quantize_mx(out=w13_codes[:, w].bitcast(FP8X4), scales=w13_plane[:, w], in_=w13_bf[:, w].rearrange("p c j -> p (c j)"))
 
+        h_codes = keep.tile([P, S], U32, name="h_codes", tag="w13_then_h", align_bytes=64)
+        h_plane = keep.tile([P, S], U8, name="h_plane", align_bytes=64)
         for c in range(chunks):
+            cols = slice(c * CHUNK, (c + 1) * CHUNK)
             h_bf = keep.tile([P, CHUNK, PACK], BF16, name="h_bf%d" % c, align_bytes=64)
             nc.scalar.activation(h_bf[:], hidden[c][:].rearrange("p t n -> p n t"), GELU)
-            h_codes = keep.tile([P, CHUNK], U32, name="h_codes%d" % c, align_bytes=64)
-            h_plane = keep.tile([P, CHUNK], U8, name="h_plane%d" % c, align_bytes=64)
-            nc.vector.quantize_mx(out=h_codes[:].bitcast(FP8X4), scales=h_plane[:], in_=h_bf[:].rearrange("p n t -> p (n t)"))
-            acc = psum.tile([P, CHUNK], F32, name="acc%d" % c)
-            codes, plane = x_operand(c)
-            nc.tensor.matmul_mx(out=acc[:], lhsT=w13_codes[:, :N].bitcast(FP8X4), lhsT_scale=w13_plane[:, :N],
-                                rhs=codes, rhs_scale=plane, start=True, stop=False)
-            nc.tensor.matmul_mx(out=acc[:], lhsT=w13_codes[:, N:].bitcast(FP8X4), lhsT_scale=w13_plane[:, N:],
-                                rhs=h_codes[:].bitcast(FP8X4), rhs_scale=h_plane[:], start=False, stop=True)
-            result = keep.tile([P, CHUNK], F32, name="result%d" % c)
-            if c == chunks - 2:
+            nc.vector.quantize_mx(out=h_codes[:, cols].bitcast(FP8X4), scales=h_plane[:, cols], in_=h_bf[:].rearrange("p n t -> p (n t)"))
+
+        for lo, hi in OUT_PIECES:
+            g, first = divmod(lo, GATHER)
+            acc = psum.tile([P, hi - lo], F32, name="acc%d" % lo)
+            nc.tensor.matmul_mx(out=acc[:], lhsT=w13_codes[:, 0].bitcast(FP8X4), lhsT_scale=w13_plane[:, 0],
+                                rhs=x_codes[g][:, first : first + hi - lo].bitcast(FP8X4), rhs_scale=x_plane[:, lo:hi], start=True, stop=False)
+            nc.tensor.matmul_mx(out=acc[:], lhsT=w13_codes[:, 1].bitcast(FP8X4), lhsT_scale=w13_plane[:, 1],
+                                rhs=h_codes[:, lo:hi].bitcast(FP8X4), rhs_scale=h_plane[:, lo:hi], start=False, stop=True)
+            result = keep.tile([P, hi - lo], F32, name="result%d" % lo)
+            if hi < S:
                 nc.scalar.copy(result[:], acc[:])
             else:
                 nc.vector.tensor_copy(result[:], acc[:])
-            nc.sync.dma_start(out[:, c * CHUNK : (c + 1) * CHUNK], result[:])
+            nc.sync.dma_start(out[:, lo:hi], result[:])

@@ -20,6 +20,8 @@ GATHER = 256
 CHUNK = 128
 W2_SCALAR = 48
 W2_FIRST = 768
+WARM_PASSES = 6
+WARM_M = 32
 OUT_PIECES = ((0, 256), (256, 384), (384, 512))
 
 
@@ -54,6 +56,16 @@ def tile_picked_phlora_gelu_p_kernel(tc, x_words, x_scales, w1, w2, w3, offs, ou
         nc.vector.tensor_copy(picked_scales[:], scale_table[:].indirect(lists[:]))
         for r in range(4):
             nc.sync.dma_start(x_plane[r:P:32, :].bitcast(I32), picked_scales[8 * r : P : 32, :].bitcast(I32))
+
+        zeros_bf = keep.tile([P, PACK * S], BF16, name="zeros_bf", align_bytes=64)
+        nc.vector.memset(zeros_bf[:].bitcast(I32), 0)
+        zero_codes = keep.tile([P, S], U32, name="zero_codes", align_bytes=64)
+        zero_plane = keep.tile([P, S], U8, name="zero_plane", align_bytes=64)
+        nc.vector.quantize_mx(out=zero_codes[:].bitcast(FP8X4), scales=zero_plane[:], in_=zeros_bf[:])
+        warm_bank = psum.tile([WARM_M, S], F32, name="warm_bank")
+        for i in range(WARM_PASSES):
+            nc.tensor.matmul_mx(out=warm_bank[:], lhsT=zero_codes[:, :WARM_M].bitcast(FP8X4), lhsT_scale=zero_plane[:, :WARM_M],
+                                rhs=zero_codes[:].bitcast(FP8X4), rhs_scale=picked_scales[:], start=True, stop=True)
 
         w13_raw = keep.tile([P, 2, PACK, N], F32, name="w13_raw", tag="early_late", align_bytes=64)
         nc.sync.dma_start(w13_raw[:, 0], w1.rearrange("(p j) c -> p j c", j=PACK))

@@ -53,7 +53,9 @@ def tile_picked_phlora_gelu_p_kernel(tc, x_words, x_scales, w1, w2, w3, offs, ou
         nc.scalar.activation(warm_out[:], warm_in[:], GELU)
 
         picked_scales = keep.tile([P, S], U8, name="picked_scales", align_bytes=64)
-        nc.vector.tensor_copy(picked_scales[:], scale_table[:].indirect(lists[:]))
+        for g in range(S // GATHER):
+            cols = GATHER // 16
+            nc.vector.tensor_copy(picked_scales[:, g * GATHER : (g + 1) * GATHER], scale_table[:].indirect(lists[:, g * cols : (g + 1) * cols]))
         for r in range(4):
             nc.sync.dma_start(x_plane[r:P:32, :].bitcast(I32), picked_scales[8 * r : P : 32, :].bitcast(I32))
 
@@ -64,8 +66,8 @@ def tile_picked_phlora_gelu_p_kernel(tc, x_words, x_scales, w1, w2, w3, offs, ou
         nc.vector.quantize_mx(out=zero_codes[:].bitcast(FP8X4), scales=zero_plane[:], in_=zeros_bf[:])
         warm_bank = psum.tile([WARM_M, S], F32, name="warm_bank")
         for i in range(WARM_PASSES):
-            nc.tensor.matmul_mx(out=warm_bank[:], lhsT=zero_codes[:, :WARM_M].bitcast(FP8X4), lhsT_scale=zero_plane[:, :WARM_M],
-                                rhs=zero_codes[:].bitcast(FP8X4), rhs_scale=picked_scales[:], start=True, stop=True)
+            nc.tensor.matmul_mx(out=warm_bank[:], lhsT=zero_codes[:, :WARM_M].bitcast(FP8X4), lhsT_scale=picked_scales[:, :WARM_M],
+                                rhs=zero_codes[:].bitcast(FP8X4), rhs_scale=zero_plane[:], start=True, stop=True)
 
         w13_raw = keep.tile([P, 2, PACK, N], F32, name="w13_raw", tag="early_late", align_bytes=64)
         nc.sync.dma_start(w13_raw[:, 0], w1.rearrange("(p j) c -> p j c", j=PACK))

@@ -22,6 +22,7 @@ W2_SCALAR = 48
 W2_FIRST = 768
 WARM_PASSES = 6
 WARM_M = 32
+H_PIECES = ((0, 128), (128, 256), (256, 384), (384, 448), (448, 512))
 OUT_PIECES = ((0, 256), (256, 384), (384, 512))
 
 
@@ -29,9 +30,10 @@ def tile_picked_phlora_gelu_p_kernel(tc, x_words, x_scales, w1, w2, w3, offs, ou
     nc = tc.nc
     with ExitStack() as ctx:
         keep = ctx.enter_context(tc.tile_pool(name="keep", bufs=1))
+        shared = ctx.enter_context(tc.tile_pool(name="shared", bufs=1))
         psum = ctx.enter_context(tc.psum_pool(name="psum", bufs=1))
 
-        scale_table = keep.tile([P, T], U8, name="scale_table", tag="early_late", align_bytes=64)
+        scale_table = shared.tile([P, T], U8, name="scale_table", offset=T // 2)
         nc.vector.memset(scale_table[:].bitcast(I32), 0)
 
         w2_raw = keep.tile([P, PACK * H], F32, name="w2_raw")
@@ -69,9 +71,10 @@ def tile_picked_phlora_gelu_p_kernel(tc, x_words, x_scales, w1, w2, w3, offs, ou
             nc.tensor.matmul_mx(out=warm_bank[:], lhsT=zero_codes[:, :WARM_M].bitcast(FP8X4), lhsT_scale=picked_scales[:, :WARM_M],
                                 rhs=zero_codes[:].bitcast(FP8X4), rhs_scale=zero_plane[:], start=True, stop=True)
 
-        w13_raw = keep.tile([P, 2, PACK, N], F32, name="w13_raw", tag="early_late", align_bytes=64)
-        nc.sync.dma_start(w13_raw[:, 0], w1.rearrange("(p j) c -> p j c", j=PACK))
-        nc.sync.dma_start(w13_raw[:, 1], w3.rearrange("(p j) c -> p j c", j=PACK))
+        w1_raw = shared.tile([P, PACK, N], F32, name="w1_raw", offset=0)
+        w3_raw = shared.tile([P, PACK, N], F32, name="w3_raw", offset=T)
+        nc.sync.dma_start(w1_raw[:], w1.rearrange("(p j) c -> p j c", j=PACK))
+        nc.sync.dma_start(w3_raw[:], w3.rearrange("(p j) c -> p j c", j=PACK))
 
         w2_bf = keep.tile([P, PACK, P, PACK], BF16, name="w2_bf", align_bytes=64)
         w2_dst = w2_bf[:].rearrange("p t m j -> p m t j")
@@ -107,17 +110,18 @@ def tile_picked_phlora_gelu_p_kernel(tc, x_words, x_scales, w1, w2, w3, offs, ou
         w13_bf = keep.tile([P, 2, N, PACK], BF16, name="w13_bf", tag="w13_then_h", align_bytes=64)
         w13_codes = keep.tile([P, 2, N], U32, name="w13_codes", align_bytes=64)
         w13_plane = keep.tile([P, 2, N], U8, name="w13_plane", align_bytes=64)
-        for w in range(2):
-            nc.vector.tensor_copy(w13_bf[:, w].rearrange("p (c i) j -> p c j i", i=4), w13_raw[:, w].rearrange("p j (c i) -> p c j i", i=4))
+        nc.vector.tensor_copy(w13_bf[:, 0].rearrange("p (c i) j -> p c j i", i=4), w1_raw[:].rearrange("p j (c i) -> p c j i", i=4))
+        nc.vector.tensor_copy(w13_bf[:, 1].rearrange("p (c i) j -> p c j i", i=4), w3_raw[:].rearrange("p j (c i) -> p c j i", i=4))
         for w in range(2):
             nc.vector.quantize_mx(out=w13_codes[:, w].bitcast(FP8X4), scales=w13_plane[:, w], in_=w13_bf[:, w].rearrange("p c j -> p (c j)"))
 
         h_codes = keep.tile([P, S], U32, name="h_codes", tag="w13_then_h", align_bytes=64)
         h_plane = keep.tile([P, S], U8, name="h_plane", align_bytes=64)
-        for c in range(chunks):
-            cols = slice(c * CHUNK, (c + 1) * CHUNK)
-            h_bf = keep.tile([P, CHUNK, PACK], BF16, name="h_bf%d" % c, align_bytes=64)
-            nc.scalar.activation(h_bf[:], hidden[c][:].rearrange("p t n -> p n t"), GELU)
+        for lo, hi in H_PIECES:
+            cols = slice(lo, hi)
+            c, first = divmod(lo, CHUNK)
+            h_bf = keep.tile([P, hi - lo, PACK], BF16, name="h_bf%d" % lo, align_bytes=64)
+            nc.scalar.activation(h_bf[:], hidden[c][:, :, first : first + hi - lo].rearrange("p t n -> p n t"), GELU)
             nc.vector.quantize_mx(out=h_codes[:, cols].bitcast(FP8X4), scales=h_plane[:, cols], in_=h_bf[:].rearrange("p n t -> p (n t)"))
 
         for lo, hi in OUT_PIECES:

@@ -18,7 +18,7 @@ P = 128
 PACK = 4
 GATHER = 256
 CHUNK = 128
-W2_SCALAR = 48
+W2_SCALAR = 40
 W2_FIRST = 768
 WARM_PASSES = 6
 WARM_M = 32
@@ -80,10 +80,15 @@ def tile_picked_phlora_gelu_p_kernel(tc, x_words, x_scales, w1, w2, w3, offs, ou
         w2_dst = w2_bf[:].rearrange("p t m j -> p m t j")
         w2_src = w2_raw[:].rearrange("p (j m t) -> p m t j", j=PACK, t=PACK)
         nc.scalar.copy(w2_dst[:, :W2_SCALAR], w2_src[:, :W2_SCALAR])
-        nc.vector.tensor_copy(w2_dst[:, W2_SCALAR:], w2_src[:, W2_SCALAR:])
+        half = P // 2
+        nc.vector.tensor_copy(w2_dst[:, half:], w2_src[:, half:])
+        nc.vector.tensor_copy(w2_dst[:, W2_SCALAR:half], w2_src[:, W2_SCALAR:half])
         w2_codes = keep.tile([P, H], U32, name="w2_codes", align_bytes=64)
         w2_plane = keep.tile([P, H], U8, name="w2_plane", align_bytes=64)
-        nc.vector.quantize_mx(out=w2_codes[:].bitcast(FP8X4), scales=w2_plane[:], in_=w2_bf[:].rearrange("p t m j -> p (t m j)"))
+        for lo in (half, 0):
+            for t in range(PACK):
+                cols = slice(t * P + lo, t * P + lo + half)
+                nc.vector.quantize_mx(out=w2_codes[:, cols].bitcast(FP8X4), scales=w2_plane[:, cols], in_=w2_bf[:, t, lo : lo + half, :].rearrange("p m j -> p (m j)"))
 
         x_codes = []
         for g in range(S // GATHER):

@@ -20,7 +20,7 @@ GATHER = 256
 CHUNK = 128
 W2_SCALAR = 40
 W2_FIRST = 768
-WARM_PASSES = 6
+WARM_PASSES = 2
 WARM_M = 32
 H_PIECES = ((0, 128), (128, 256), (256, 384), (384, 448), (448, 512))
 OUT_PIECES = ((0, 256), (256, 384), (384, 512))
@@ -68,7 +68,7 @@ def tile_picked_phlora_gelu_p_kernel(tc, x_words, x_scales, w1, w2, w3, offs, ou
         nc.vector.quantize_mx(out=zero_codes[:].bitcast(FP8X4), scales=zero_plane[:], in_=zeros_bf[:])
         warm_bank = psum.tile([WARM_M, S], F32, name="warm_bank")
         for i in range(WARM_PASSES):
-            nc.tensor.matmul_mx(out=warm_bank[:], lhsT=zero_codes[:, :WARM_M].bitcast(FP8X4), lhsT_scale=picked_scales[:, :WARM_M],
+            nc.tensor.matmul_mx(out=warm_bank[:], lhsT=zero_codes[:, :WARM_M].bitcast(FP8X4), lhsT_scale=picked_scales[:, GATHER : GATHER + WARM_M],
                                 rhs=zero_codes[:].bitcast(FP8X4), rhs_scale=zero_plane[:], start=True, stop=True)
 
         w1_raw = shared.tile([P, PACK, N], F32, name="w1_raw", offset=0)
@@ -79,16 +79,14 @@ def tile_picked_phlora_gelu_p_kernel(tc, x_words, x_scales, w1, w2, w3, offs, ou
         w2_bf = keep.tile([P, PACK, P, PACK], BF16, name="w2_bf", align_bytes=64)
         w2_dst = w2_bf[:].rearrange("p t m j -> p m t j")
         w2_src = w2_raw[:].rearrange("p (j m t) -> p m t j", j=PACK, t=PACK)
-        nc.scalar.copy(w2_dst[:, :W2_SCALAR], w2_src[:, :W2_SCALAR])
-        half = P // 2
-        nc.vector.tensor_copy(w2_dst[:, half:], w2_src[:, half:])
-        nc.vector.tensor_copy(w2_dst[:, W2_SCALAR:half], w2_src[:, W2_SCALAR:half])
+        for t in range(0, PACK, 2):
+            nc.scalar.copy(w2_dst[:, :W2_SCALAR, t : t + 2], w2_src[:, :W2_SCALAR, t : t + 2])
+            nc.vector.tensor_copy(w2_dst[:, W2_SCALAR:, t : t + 2], w2_src[:, W2_SCALAR:, t : t + 2])
         w2_codes = keep.tile([P, H], U32, name="w2_codes", align_bytes=64)
         w2_plane = keep.tile([P, H], U8, name="w2_plane", align_bytes=64)
-        for lo in (half, 0):
-            for t in range(PACK):
-                cols = slice(t * P + lo, t * P + lo + half)
-                nc.vector.quantize_mx(out=w2_codes[:, cols].bitcast(FP8X4), scales=w2_plane[:, cols], in_=w2_bf[:, t, lo : lo + half, :].rearrange("p m j -> p (m j)"))
+        for t in range(0, PACK, 2):
+            cols = slice(t * P, (t + 2) * P)
+            nc.vector.quantize_mx(out=w2_codes[:, cols].bitcast(FP8X4), scales=w2_plane[:, cols], in_=w2_bf[:, t : t + 2].rearrange("p t m j -> p (t m j)"))
 
         x_codes = []
         for g in range(S // GATHER):
@@ -137,8 +135,5 @@ def tile_picked_phlora_gelu_p_kernel(tc, x_words, x_scales, w1, w2, w3, offs, ou
             nc.tensor.matmul_mx(out=acc[:], lhsT=w13_codes[:, 1].bitcast(FP8X4), lhsT_scale=w13_plane[:, 1],
                                 rhs=h_codes[:, lo:hi].bitcast(FP8X4), rhs_scale=h_plane[:, lo:hi], start=False, stop=True)
             result = keep.tile([P, hi - lo], F32, name="result%d" % lo)
-            if hi < S:
-                nc.scalar.copy(result[:], acc[:])
-            else:
-                nc.vector.tensor_copy(result[:], acc[:])
+            nc.scalar.copy(result[:], acc[:])
             nc.sync.dma_start(out[:, lo:hi], result[:])

@@ -18,12 +18,13 @@ P = 128
 PACK = 4
 GATHER = 256
 CHUNK = 128
-W2_SCALAR = 40
+W2_SCALAR = 32
 W2_FIRST = 768
 WARM_PASSES = 2
 WARM_M = 32
-H_PIECES = ((0, 128), (128, 256), (256, 384), (384, 448), (448, 512))
-OUT_PIECES = ((0, 256), (256, 384), (384, 512))
+PAIRED = 1
+H_PIECES = ((128, 256), (256, 384), (384, 448), (448, 512))
+STORES = ((0, 256), (256, 384), (384, 512))
 
 
 def tile_picked_phlora_gelu_p_kernel(tc, x_words, x_scales, w1, w2, w3, offs, out):
@@ -66,11 +67,6 @@ def tile_picked_phlora_gelu_p_kernel(tc, x_words, x_scales, w1, w2, w3, offs, ou
         zero_codes = keep.tile([P, S], U32, name="zero_codes", align_bytes=64)
         zero_plane = keep.tile([P, S], U8, name="zero_plane", align_bytes=64)
         nc.vector.quantize_mx(out=zero_codes[:].bitcast(FP8X4), scales=zero_plane[:], in_=zeros_bf[:])
-        warm_bank = psum.tile([WARM_M, S], F32, name="warm_bank")
-        for i in range(WARM_PASSES):
-            nc.tensor.matmul_mx(out=warm_bank[:], lhsT=zero_codes[:, :WARM_M].bitcast(FP8X4), lhsT_scale=picked_scales[:, GATHER : GATHER + WARM_M],
-                                rhs=zero_codes[:].bitcast(FP8X4), rhs_scale=zero_plane[:], start=True, stop=True)
-
         w1_raw = shared.tile([P, PACK, N], F32, name="w1_raw", offset=0)
         w3_raw = shared.tile([P, PACK, N], F32, name="w3_raw", offset=T)
         nc.sync.dma_start(w1_raw[:], w1.rearrange("(p j) c -> p j c", j=PACK))
@@ -79,14 +75,32 @@ def tile_picked_phlora_gelu_p_kernel(tc, x_words, x_scales, w1, w2, w3, offs, ou
         w2_bf = keep.tile([P, PACK, P, PACK], BF16, name="w2_bf", align_bytes=64)
         w2_dst = w2_bf[:].rearrange("p t m j -> p m t j")
         w2_src = w2_raw[:].rearrange("p (j m t) -> p m t j", j=PACK, t=PACK)
-        for t in range(0, PACK, 2):
-            nc.scalar.copy(w2_dst[:, :W2_SCALAR, t : t + 2], w2_src[:, :W2_SCALAR, t : t + 2])
-            nc.vector.tensor_copy(w2_dst[:, W2_SCALAR:, t : t + 2], w2_src[:, W2_SCALAR:, t : t + 2])
+        nc.scalar.copy(w2_dst[:, :W2_SCALAR], w2_src[:, :W2_SCALAR])
+        half, early = P // 2, P // 2 + WARM_M
         w2_codes = keep.tile([P, H], U32, name="w2_codes", align_bytes=64)
         w2_plane = keep.tile([P, H], U8, name="w2_plane", align_bytes=64)
-        for t in range(0, PACK, 2):
-            cols = slice(t * P, (t + 2) * P)
-            nc.vector.quantize_mx(out=w2_codes[:, cols].bitcast(FP8X4), scales=w2_plane[:, cols], in_=w2_bf[:, t : t + 2].rearrange("p t m j -> p (t m j)"))
+
+        def round_w2(lo, hi):
+            nc.vector.tensor_copy(w2_dst[:, lo:hi], w2_src[:, lo:hi])
+
+        def quantize_w2(t, lo, hi):
+            cols = slice(t * P + lo, t * P + hi)
+            nc.vector.quantize_mx(out=w2_codes[:, cols].bitcast(FP8X4), scales=w2_plane[:, cols], in_=w2_bf[:, t, lo:hi, :].rearrange("p m j -> p (m j)"))
+
+        round_w2(half, early)
+        round_w2(W2_SCALAR, half)
+        quantize_w2(0, half, early)
+        round_w2(early, P)
+        for t in range(PACK):
+            quantize_w2(t, 0, half)
+        quantize_w2(0, early, P)
+        for t in range(1, PACK):
+            quantize_w2(t, half, P)
+
+        warm_bank = psum.tile([WARM_M, S], F32, name="warm_bank", tag="hidden3_0")
+        for i in range(WARM_PASSES):
+            nc.tensor.matmul_mx(out=warm_bank[:], lhsT=w2_codes[:, half:early].bitcast(FP8X4), lhsT_scale=w2_plane[:, half:early],
+                                rhs=zero_codes[:].bitcast(FP8X4), rhs_scale=zero_plane[:], start=True, stop=True)
 
         x_codes = []
         for g in range(S // GATHER):
@@ -99,18 +113,21 @@ def tile_picked_phlora_gelu_p_kernel(tc, x_words, x_scales, w1, w2, w3, offs, ou
             g, lo = divmod(c * CHUNK, GATHER)
             return x_codes[g][:, lo : lo + CHUNK].bitcast(FP8X4), x_plane[:, c * CHUNK : (c + 1) * CHUNK]
 
-        chunks = S // CHUNK
         hidden = []
-        for c in range(chunks):
-            bank = psum.tile([P, PACK, CHUNK], F32, name="hidden%d" % c)
+        for c in range(S // CHUNK):
             codes, plane = x_operand(c)
-            for t in range(PACK):
-                cols = slice(t * P, (t + 1) * P)
-                nc.tensor.matmul_mx(out=bank[:, t, :], lhsT=w2_codes[:, cols].bitcast(FP8X4), lhsT_scale=w2_plane[:, cols],
-                                    rhs=codes, rhs_scale=plane, start=True, stop=True)
-            hidden.append(bank)
+            width = 2 if c < PAIRED else PACK
+            banks = []
+            for first in range(0, PACK, width):
+                bank = psum.tile([P, width, CHUNK], F32, name="hidden%d_%d" % (c, first))
+                for t in range(width):
+                    cols = slice((first + t) * P, (first + t + 1) * P)
+                    nc.tensor.matmul_mx(out=bank[:, t, :], lhsT=w2_codes[:, cols].bitcast(FP8X4), lhsT_scale=w2_plane[:, cols],
+                                        rhs=codes, rhs_scale=plane, start=True, stop=True)
+                banks.append(bank)
+            hidden.append(banks)
 
-        w13_bf = keep.tile([P, 2, N, PACK], BF16, name="w13_bf", tag="w13_then_h", align_bytes=64)
+        w13_bf = keep.tile([P, 2, N, PACK], BF16, name="w13_bf", align_bytes=64)
         w13_codes = keep.tile([P, 2, N], U32, name="w13_codes", align_bytes=64)
         w13_plane = keep.tile([P, 2, N], U8, name="w13_plane", align_bytes=64)
         nc.vector.tensor_copy(w13_bf[:, 0].rearrange("p (c i) j -> p c j i", i=4), w1_raw[:].rearrange("p j (c i) -> p c j i", i=4))
@@ -118,22 +135,36 @@ def tile_picked_phlora_gelu_p_kernel(tc, x_words, x_scales, w1, w2, w3, offs, ou
         for w in range(2):
             nc.vector.quantize_mx(out=w13_codes[:, w].bitcast(FP8X4), scales=w13_plane[:, w], in_=w13_bf[:, w].rearrange("p c j -> p (c j)"))
 
-        h_codes = keep.tile([P, S], U32, name="h_codes", tag="w13_then_h", align_bytes=64)
+        h_codes = shared.tile([P, S], U32, name="h_codes", offset=T, align_bytes=64)
         h_plane = keep.tile([P, S], U8, name="h_plane", align_bytes=64)
+        for c in range(PAIRED):
+            cols = slice(c * CHUNK, (c + 1) * CHUNK)
+            pairs = keep.tile([P, 2, CHUNK * 2], BF16, name="pairs%d" % c, align_bytes=64)
+            for u in range(2):
+                nc.scalar.activation(pairs[:, u].rearrange("p (n t) -> p n t", t=2), hidden[c][u][:].rearrange("p t n -> p n t"), GELU)
+            h_bf = keep.tile([P, CHUNK * PACK], BF16, name="h_woven%d" % c, align_bytes=64)
+            nc.vector.tensor_copy(h_bf[:].bitcast(I32).rearrange("p (n u) -> p n u", u=2), pairs[:].bitcast(I32).rearrange("p u n -> p n u"))
+            nc.vector.quantize_mx(out=h_codes[:, cols].bitcast(FP8X4), scales=h_plane[:, cols], in_=h_bf[:])
         for lo, hi in H_PIECES:
             cols = slice(lo, hi)
             c, first = divmod(lo, CHUNK)
             h_bf = keep.tile([P, hi - lo, PACK], BF16, name="h_bf%d" % lo, align_bytes=64)
-            nc.scalar.activation(h_bf[:], hidden[c][:, :, first : first + hi - lo].rearrange("p t n -> p n t"), GELU)
+            nc.scalar.activation(h_bf[:], hidden[c][0][:, :, first : first + hi - lo].rearrange("p t n -> p n t"), GELU)
             nc.vector.quantize_mx(out=h_codes[:, cols].bitcast(FP8X4), scales=h_plane[:, cols], in_=h_bf[:].rearrange("p n t -> p (n t)"))
 
-        for lo, hi in OUT_PIECES:
-            g, first = divmod(lo, GATHER)
-            acc = psum.tile([P, hi - lo], F32, name="acc%d" % lo)
-            nc.tensor.matmul_mx(out=acc[:], lhsT=w13_codes[:, 0].bitcast(FP8X4), lhsT_scale=w13_plane[:, 0],
-                                rhs=x_codes[g][:, first : first + hi - lo].bitcast(FP8X4), rhs_scale=x_plane[:, lo:hi], start=True, stop=False)
-            nc.tensor.matmul_mx(out=acc[:], lhsT=w13_codes[:, 1].bitcast(FP8X4), lhsT_scale=w13_plane[:, 1],
-                                rhs=h_codes[:, lo:hi].bitcast(FP8X4), rhs_scale=h_plane[:, lo:hi], start=False, stop=True)
+        for lo, hi in STORES:
             result = keep.tile([P, hi - lo], F32, name="result%d" % lo)
-            nc.scalar.copy(result[:], acc[:])
+            for c in range(lo // CHUNK, hi // CHUNK):
+                codes, plane = x_operand(c)
+                cols = slice(c * CHUNK, (c + 1) * CHUNK)
+                acc = psum.tile([P, CHUNK], F32, name="acc%d" % c, tag="hidden0_0" if c == 0 else "acc%d" % c)
+                nc.tensor.matmul_mx(out=acc[:], lhsT=w13_codes[:, 0].bitcast(FP8X4), lhsT_scale=w13_plane[:, 0],
+                                    rhs=codes, rhs_scale=plane, start=True, stop=False)
+                nc.tensor.matmul_mx(out=acc[:], lhsT=w13_codes[:, 1].bitcast(FP8X4), lhsT_scale=w13_plane[:, 1],
+                                    rhs=h_codes[:, cols].bitcast(FP8X4), rhs_scale=h_plane[:, cols], start=False, stop=True)
+                part = result[:, c * CHUNK - lo : (c + 1) * CHUNK - lo]
+                if hi < S:
+                    nc.scalar.copy(part, acc[:])
+                else:
+                    nc.vector.tensor_copy(part, acc[:])
             nc.sync.dma_start(out[:, lo:hi], result[:])

@@ -50,11 +50,6 @@ def tile_picked_phlora_gelu_p_kernel(tc, x_words, x_scales, w1, w2, w3, offs, ou
         x_plane = keep.tile([P, S], U8, name="x_plane", align_bytes=64)
         nc.vector.memset(x_plane[:].bitcast(I32), 0)
 
-        warm_in = keep.tile([P, 1], F32, name="warm_in")
-        warm_out = keep.tile([P, 1], F32, name="warm_out")
-        nc.vector.memset(warm_in[:], 0.0)
-        nc.scalar.activation(warm_out[:], warm_in[:], GELU)
-
         picked_scales = keep.tile([P, S], U8, name="picked_scales", align_bytes=64)
         for g in range(S // GATHER):
             cols = GATHER // 16
@@ -64,6 +59,8 @@ def tile_picked_phlora_gelu_p_kernel(tc, x_words, x_scales, w1, w2, w3, offs, ou
 
         zeros_bf = keep.tile([P, PACK * S], BF16, name="zeros_bf", align_bytes=64)
         nc.vector.memset(zeros_bf[:].bitcast(I32), 0)
+        warm_out = keep.tile([P, 1], F32, name="warm_out")
+        nc.scalar.activation(warm_out[:], zeros_bf[:, 0:1], GELU)
         zero_codes = keep.tile([P, S], U32, name="zero_codes", align_bytes=64)
         zero_plane = keep.tile([P, S], U8, name="zero_plane", align_bytes=64)
         nc.vector.quantize_mx(out=zero_codes[:].bitcast(FP8X4), scales=zero_plane[:], in_=zeros_bf[:])
@@ -87,9 +84,10 @@ def tile_picked_phlora_gelu_p_kernel(tc, x_words, x_scales, w1, w2, w3, offs, ou
             cols = slice(t * P + lo, t * P + hi)
             nc.vector.quantize_mx(out=w2_codes[:, cols].bitcast(FP8X4), scales=w2_plane[:, cols], in_=w2_bf[:, t, lo:hi, :].rearrange("p m j -> p (m j)"))
 
-        round_w2(half, early)
+        nc.vector.tensor_copy(w2_dst[:, half:early, 0:2], w2_src[:, half:early, 0:2])
         round_w2(W2_SCALAR, half)
         quantize_w2(0, half, early)
+        nc.vector.tensor_copy(w2_dst[:, half:early, 2:4], w2_src[:, half:early, 2:4])
         round_w2(early, P)
         for t in range(PACK):
             quantize_w2(t, 0, half)

@@ -47,6 +47,9 @@ def tile_picked_phlora_gelu_p_kernel(tc, x_words, x_scales, w1, w2, w3, offs, ou
         word_table = keep.tile([P, T], U32, name="word_table", align_bytes=64)
         nc.sync.dma_start(word_table[:].bitcast(I32), x_words[0].rearrange("p n t -> p (n t)").bitcast(I32))
 
+        w1_raw = keep.tile([P, PACK, N], F32, name="w1_raw")
+        nc.sync.dma_start(w1_raw[:], w1.rearrange("(p j) c -> p j c", j=PACK))
+
         x_plane = keep.tile([P, S], U8, name="x_plane", align_bytes=64)
         nc.vector.memset(x_plane[:].bitcast(I32), 0)
 
@@ -64,9 +67,7 @@ def tile_picked_phlora_gelu_p_kernel(tc, x_words, x_scales, w1, w2, w3, offs, ou
         zero_codes = keep.tile([P, S], U32, name="zero_codes", align_bytes=64)
         zero_plane = keep.tile([P, S], U8, name="zero_plane", align_bytes=64)
         nc.vector.quantize_mx(out=zero_codes[:].bitcast(FP8X4), scales=zero_plane[:], in_=zeros_bf[:])
-        w1_raw = shared.tile([P, PACK, N], F32, name="w1_raw", offset=0)
         w3_raw = shared.tile([P, PACK, N], F32, name="w3_raw", offset=T)
-        nc.sync.dma_start(w1_raw[:], w1.rearrange("(p j) c -> p j c", j=PACK))
         nc.sync.dma_start(w3_raw[:], w3.rearrange("(p j) c -> p j c", j=PACK))
 
         w2_bf = keep.tile([P, PACK, P, PACK], BF16, name="w2_bf", align_bytes=64)
@@ -128,7 +129,7 @@ def tile_picked_phlora_gelu_p_kernel(tc, x_words, x_scales, w1, w2, w3, offs, ou
         w13_bf = keep.tile([P, 2, N, PACK], BF16, name="w13_bf", align_bytes=64)
         w13_codes = keep.tile([P, 2, N], U32, name="w13_codes", align_bytes=64)
         w13_plane = keep.tile([P, 2, N], U8, name="w13_plane", align_bytes=64)
-        nc.vector.tensor_copy(w13_bf[:, 0].rearrange("p (c i) j -> p c j i", i=4), w1_raw[:].rearrange("p j (c i) -> p c j i", i=4))
+        nc.scalar.copy(w13_bf[:, 0].rearrange("p (c i) j -> p c j i", i=4), w1_raw[:].rearrange("p j (c i) -> p c j i", i=4))
         nc.vector.tensor_copy(w13_bf[:, 1].rearrange("p (c i) j -> p c j i", i=4), w3_raw[:].rearrange("p j (c i) -> p c j i", i=4))
         for w in range(2):
             nc.vector.quantize_mx(out=w13_codes[:, w].bitcast(FP8X4), scales=w13_plane[:, w], in_=w13_bf[:, w].rearrange("p c j -> p (c j)"))

@@ -18,7 +18,7 @@ P = 128
 PACK = 4
 GATHER = 256
 CHUNK = 128
-W2_SCALAR = 32
+W2_SCALAR = 64
 W2_FIRST = 768
 WARM_PASSES = 2
 WARM_M = 32
@@ -60,13 +60,8 @@ def tile_picked_phlora_gelu_p_kernel(tc, x_words, x_scales, w1, w2, w3, offs, ou
         for r in range(4):
             nc.sync.dma_start(x_plane[r:P:32, :].bitcast(I32), picked_scales[8 * r : P : 32, :].bitcast(I32))
 
-        zeros_bf = keep.tile([P, PACK * S], BF16, name="zeros_bf", align_bytes=64)
-        nc.vector.memset(zeros_bf[:].bitcast(I32), 0)
         warm_out = keep.tile([P, 1], F32, name="warm_out")
-        nc.scalar.activation(warm_out[:], zeros_bf[:, 0:1], GELU)
-        zero_codes = keep.tile([P, S], U32, name="zero_codes", align_bytes=64)
-        zero_plane = keep.tile([P, S], U8, name="zero_plane", align_bytes=64)
-        nc.vector.quantize_mx(out=zero_codes[:].bitcast(FP8X4), scales=zero_plane[:], in_=zeros_bf[:])
+        nc.scalar.activation(warm_out[:], w2_raw[:, 0:1], GELU)
         w3_raw = shared.tile([P, PACK, N], F32, name="w3_raw", offset=T)
         nc.sync.dma_start(w3_raw[:], w3.rearrange("(p j) c -> p j c", j=PACK))
 
@@ -85,21 +80,26 @@ def tile_picked_phlora_gelu_p_kernel(tc, x_words, x_scales, w1, w2, w3, offs, ou
             cols = slice(t * P + lo, t * P + hi)
             nc.vector.quantize_mx(out=w2_codes[:, cols].bitcast(FP8X4), scales=w2_plane[:, cols], in_=w2_bf[:, t, lo:hi, :].rearrange("p m j -> p (m j)"))
 
-        nc.vector.tensor_copy(w2_dst[:, half:early, 0:2], w2_src[:, half:early, 0:2])
-        round_w2(W2_SCALAR, half)
-        quantize_w2(0, half, early)
-        nc.vector.tensor_copy(w2_dst[:, half:early, 2:4], w2_src[:, half:early, 2:4])
+        nc.vector.tensor_copy(w2_dst[:, half:early, 0], w2_src[:, half:early, 0])
         round_w2(early, P)
-        for t in range(PACK):
-            quantize_w2(t, 0, half)
+        quantize_w2(0, half, early)
+        nc.vector.tensor_copy(w2_dst[:, half:early, 1:4], w2_src[:, half:early, 1:4])
+        reps = S // WARM_M
+        warm_codes = keep.tile([P, reps, WARM_M], I32, name="warm_codes", align_bytes=64)
+        warm_plane = keep.tile([P, reps, WARM_M // 4], I32, name="warm_plane", align_bytes=64)
+        nc.vector.tensor_copy(warm_plane[:], w2_plane[:, half:early].bitcast(I32).unsqueeze(1).to_broadcast([P, reps, WARM_M // 4]))
+        nc.vector.tensor_copy(warm_codes[:], w2_codes[:, half:early].bitcast(I32).unsqueeze(1).to_broadcast([P, reps, WARM_M]))
         quantize_w2(0, early, P)
         for t in range(1, PACK):
             quantize_w2(t, half, P)
+        for t in range(PACK):
+            quantize_w2(t, 0, half)
 
         warm_bank = psum.tile([WARM_M, S], F32, name="warm_bank", tag="hidden3_0")
         for i in range(WARM_PASSES):
             nc.tensor.matmul_mx(out=warm_bank[:], lhsT=w2_codes[:, half:early].bitcast(FP8X4), lhsT_scale=w2_plane[:, half:early],
-                                rhs=zero_codes[:].bitcast(FP8X4), rhs_scale=zero_plane[:], start=True, stop=True)
+                                rhs=warm_codes[:].rearrange("p r m -> p (r m)").bitcast(FP8X4),
+                                rhs_scale=warm_plane[:].rearrange("p r m -> p (r m)").bitcast(U8), start=True, stop=True)
 
         x_codes = []
         for g in range(S // GATHER):

@@ -24,7 +24,8 @@ WARM_PASSES = 2
 WARM_M = 32
 PAIRED = 1
 H_PIECES = ((128, 256), (256, 384), (384, 448), (448, 512))
-STORES = ((0, 256), (256, 384), (384, 512))
+STORES = ((0, 256), (256, 384))
+NARROW = 64
 
 
 def tile_picked_phlora_gelu_p_kernel(tc, x_words, x_scales, w1, w2, w3, offs, out):
@@ -54,9 +55,7 @@ def tile_picked_phlora_gelu_p_kernel(tc, x_words, x_scales, w1, w2, w3, offs, ou
         nc.vector.memset(x_plane[:].bitcast(I32), 0)
 
         picked_scales = keep.tile([P, S], U8, name="picked_scales", align_bytes=64)
-        for g in range(S // GATHER):
-            cols = GATHER // 16
-            nc.vector.tensor_copy(picked_scales[:, g * GATHER : (g + 1) * GATHER], scale_table[:].indirect(lists[:, g * cols : (g + 1) * cols]))
+        nc.vector.tensor_copy(picked_scales[:], scale_table[:].indirect(lists[:]))
         for r in range(4):
             nc.sync.dma_start(x_plane[r:P:32, :].bitcast(I32), picked_scales[8 * r : P : 32, :].bitcast(I32))
 
@@ -134,6 +133,14 @@ def tile_picked_phlora_gelu_p_kernel(tc, x_words, x_scales, w1, w2, w3, offs, ou
         for w in range(2):
             nc.vector.quantize_mx(out=w13_codes[:, w].bitcast(FP8X4), scales=w13_plane[:, w], in_=w13_bf[:, w].rearrange("p c j -> p (c j)"))
 
+        last = S - CHUNK
+        codes, plane = x_operand(last // CHUNK)
+        base_bank = psum.tile([P, CHUNK], F32, name="base_bank")
+        nc.tensor.matmul_mx(out=base_bank[:], lhsT=w13_codes[:, 0].bitcast(FP8X4), lhsT_scale=w13_plane[:, 0],
+                            rhs=codes, rhs_scale=plane, start=True, stop=True)
+        base = keep.tile([P, CHUNK], F32, name="base")
+        nc.vector.tensor_copy(base[:], base_bank[:])
+
         h_codes = shared.tile([P, S], U32, name="h_codes", offset=T, align_bytes=64)
         h_plane = keep.tile([P, S], U8, name="h_plane", align_bytes=64)
         for c in range(PAIRED):
@@ -162,8 +169,14 @@ def tile_picked_phlora_gelu_p_kernel(tc, x_words, x_scales, w1, w2, w3, offs, ou
                 nc.tensor.matmul_mx(out=acc[:], lhsT=w13_codes[:, 1].bitcast(FP8X4), lhsT_scale=w13_plane[:, 1],
                                     rhs=h_codes[:, cols].bitcast(FP8X4), rhs_scale=h_plane[:, cols], start=False, stop=True)
                 part = result[:, c * CHUNK - lo : (c + 1) * CHUNK - lo]
-                if hi < S:
-                    nc.scalar.copy(part, acc[:])
-                else:
-                    nc.vector.tensor_copy(part, acc[:])
+                nc.scalar.copy(part, acc[:])
             nc.sync.dma_start(out[:, lo:hi], result[:])
+
+        result = keep.tile([P, CHUNK], F32, name="result_last")
+        for lo, tag in ((0, "hidden0_2"), (NARROW, "hidden1_0")):
+            cols = slice(last + lo, last + lo + NARROW)
+            acc = psum.tile([P, NARROW], F32, name="acc_last%d" % lo, tag=tag)
+            nc.tensor.matmul_mx(out=acc[:], lhsT=w13_codes[:, 1].bitcast(FP8X4), lhsT_scale=w13_plane[:, 1],
+                                rhs=h_codes[:, cols].bitcast(FP8X4), rhs_scale=h_plane[:, cols], start=True, stop=True)
+            nc.vector.tensor_tensor(result[:, lo : lo + NARROW], acc[:], base[:, lo : lo + NARROW], mybir.AluOpType.add)
+        nc.sync.dma_start(out[:, last:], result[:])

@@ -59,8 +59,12 @@ def tile_picked_phlora_gelu_p_kernel(tc, x_words, x_scales, w1, w2, w3, offs, ou
         for r in range(4):
             nc.sync.dma_start(x_plane[r:P:32, :].bitcast(I32), picked_scales[8 * r : P : 32, :].bitcast(I32))
 
-        warm_out = keep.tile([P, 1], F32, name="warm_out")
-        nc.scalar.activation(warm_out[:], w2_raw[:, 0:1], GELU)
+        warm_bf = keep.tile([P, 8, 256], BF16, name="warm_bf", align_bytes=64)
+        nc.scalar.activation(warm_bf[:, 0:5], w2_raw[:, 0:256].unsqueeze(1).to_broadcast([P, 5, 256]), GELU)
+        nc.vector.tensor_copy(warm_bf[:, 5:8], w2_raw[:, 0:768].rearrange("p (r n) -> p r n", r=3))
+        warm_codes = keep.tile([P, S], U32, name="warm_codes", align_bytes=64)
+        warm_plane = keep.tile([P, S], U8, name="warm_plane", align_bytes=64)
+        nc.vector.quantize_mx(out=warm_codes[:].bitcast(FP8X4), scales=warm_plane[:], in_=warm_bf[:].rearrange("p r n -> p (r n)"))
         w3_raw = shared.tile([P, PACK, N], F32, name="w3_raw", offset=T)
         nc.sync.dma_start(w3_raw[:], w3.rearrange("(p j) c -> p j c", j=PACK))
 
@@ -68,7 +72,7 @@ def tile_picked_phlora_gelu_p_kernel(tc, x_words, x_scales, w1, w2, w3, offs, ou
         w2_dst = w2_bf[:].rearrange("p t m j -> p m t j")
         w2_src = w2_raw[:].rearrange("p (j m t) -> p m t j", j=PACK, t=PACK)
         nc.scalar.copy(w2_dst[:, :W2_SCALAR], w2_src[:, :W2_SCALAR])
-        half, early = P // 2, P // 2 + WARM_M
+        half = P // 2
         w2_codes = keep.tile([P, H], U32, name="w2_codes", align_bytes=64)
         w2_plane = keep.tile([P, H], U8, name="w2_plane", align_bytes=64)
 
@@ -79,26 +83,15 @@ def tile_picked_phlora_gelu_p_kernel(tc, x_words, x_scales, w1, w2, w3, offs, ou
             cols = slice(t * P + lo, t * P + hi)
             nc.vector.quantize_mx(out=w2_codes[:, cols].bitcast(FP8X4), scales=w2_plane[:, cols], in_=w2_bf[:, t, lo:hi, :].rearrange("p m j -> p (m j)"))
 
-        nc.vector.tensor_copy(w2_dst[:, half:early, 0], w2_src[:, half:early, 0])
-        round_w2(early, P)
-        quantize_w2(0, half, early)
-        nc.vector.tensor_copy(w2_dst[:, half:early, 1:4], w2_src[:, half:early, 1:4])
-        reps = S // WARM_M
-        warm_codes = keep.tile([P, reps, WARM_M], I32, name="warm_codes", align_bytes=64)
-        warm_plane = keep.tile([P, reps, WARM_M // 4], I32, name="warm_plane", align_bytes=64)
-        nc.vector.tensor_copy(warm_plane[:], w2_plane[:, half:early].bitcast(I32).unsqueeze(1).to_broadcast([P, reps, WARM_M // 4]))
-        nc.vector.tensor_copy(warm_codes[:], w2_codes[:, half:early].bitcast(I32).unsqueeze(1).to_broadcast([P, reps, WARM_M]))
-        quantize_w2(0, early, P)
-        for t in range(1, PACK):
-            quantize_w2(t, half, P)
-        for t in range(PACK):
-            quantize_w2(t, 0, half)
+        round_w2(half, P)
+        for lo in (0, half):
+            for t in range(PACK):
+                quantize_w2(t, lo, lo + half)
 
         warm_bank = psum.tile([WARM_M, S], F32, name="warm_bank", tag="hidden3_0")
         for i in range(WARM_PASSES):
-            nc.tensor.matmul_mx(out=warm_bank[:], lhsT=w2_codes[:, half:early].bitcast(FP8X4), lhsT_scale=w2_plane[:, half:early],
-                                rhs=warm_codes[:].rearrange("p r m -> p (r m)").bitcast(FP8X4),
-                                rhs_scale=warm_plane[:].rearrange("p r m -> p (r m)").bitcast(U8), start=True, stop=True)
+            nc.tensor.matmul_mx(out=warm_bank[:], lhsT=warm_codes[:, :WARM_M].bitcast(FP8X4), lhsT_scale=warm_plane[:, :WARM_M],
+                                rhs=warm_codes[:].bitcast(FP8X4), rhs_scale=warm_plane[:], start=True, stop=True)
 
         x_codes = []
         for g in range(S // GATHER):

@@ -19,12 +19,13 @@ PACK = 4
 GATHER = 256
 CHUNK = 128
 W2_SCALAR = 64
-W2_FIRST = 768
-WARM_PASSES = 2
+W2_FIRST = 512
+WARM_WIDTHS = (512, 512, 128)
+SEED = 32
 WARM_M = 32
 PAIRED = 1
 H_PIECES = ((128, 256), (256, 384), (384, 448), (448, 512))
-STORES = ((0, 256), (256, 384))
+STORES = ((0, 128), (128, 256), (256, 384))
 NARROW = 64
 
 
@@ -36,7 +37,8 @@ def tile_picked_phlora_gelu_p_kernel(tc, x_words, x_scales, w1, w2, w3, offs, ou
         psum = ctx.enter_context(tc.psum_pool(name="psum", bufs=1))
 
         scale_table = shared.tile([P, T], U8, name="scale_table", offset=T // 2)
-        nc.vector.memset(scale_table[:].bitcast(I32), 0)
+        nc.vector.memset(scale_table[:, : T // 2].bitcast(I32), 0)
+        nc.gpsimd.memset(scale_table[:, T // 2 :].bitcast(I32), 0)
 
         w2_raw = keep.tile([P, PACK * H], F32, name="w2_raw")
         w2_rows = w2.rearrange("(p j) c -> p (j c)", j=PACK)
@@ -59,12 +61,15 @@ def tile_picked_phlora_gelu_p_kernel(tc, x_words, x_scales, w1, w2, w3, offs, ou
         for r in range(4):
             nc.sync.dma_start(x_plane[r:P:32, :].bitcast(I32), picked_scales[8 * r : P : 32, :].bitcast(I32))
 
-        warm_bf = keep.tile([P, 8, 256], BF16, name="warm_bf", align_bytes=64)
-        nc.scalar.activation(warm_bf[:, 0:5], w2_raw[:, 0:256].unsqueeze(1).to_broadcast([P, 5, 256]), GELU)
-        nc.vector.tensor_copy(warm_bf[:, 5:8], w2_raw[:, 0:768].rearrange("p (r n) -> p r n", r=3))
+        seed_bf = keep.tile([P, PACK * SEED], BF16, name="seed_bf", align_bytes=64)
+        nc.scalar.activation(seed_bf[:], w2_raw[:, : PACK * SEED], GELU)
+        seed_codes = keep.tile([P, SEED], U32, name="seed_codes", align_bytes=64)
+        seed_plane = keep.tile([P, SEED], U8, name="seed_plane", align_bytes=64)
+        nc.vector.quantize_mx(out=seed_codes[:].bitcast(FP8X4), scales=seed_plane[:], in_=seed_bf[:])
         warm_codes = keep.tile([P, S], U32, name="warm_codes", align_bytes=64)
         warm_plane = keep.tile([P, S], U8, name="warm_plane", align_bytes=64)
-        nc.vector.quantize_mx(out=warm_codes[:].bitcast(FP8X4), scales=warm_plane[:], in_=warm_bf[:].rearrange("p r n -> p (r n)"))
+        nc.vector.tensor_copy(warm_codes[:].bitcast(I32).rearrange("p (r n) -> p r n", n=SEED),
+                              seed_codes[:].bitcast(I32).unsqueeze(1).to_broadcast([P, S // SEED, SEED]))
         w3_raw = shared.tile([P, PACK, N], F32, name="w3_raw", offset=T)
         nc.sync.dma_start(w3_raw[:], w3.rearrange("(p j) c -> p j c", j=PACK))
 
@@ -83,15 +88,23 @@ def tile_picked_phlora_gelu_p_kernel(tc, x_words, x_scales, w1, w2, w3, offs, ou
             cols = slice(t * P + lo, t * P + hi)
             nc.vector.quantize_mx(out=w2_codes[:, cols].bitcast(FP8X4), scales=w2_plane[:, cols], in_=w2_bf[:, t, lo:hi, :].rearrange("p m j -> p (m j)"))
 
-        round_w2(half, P)
-        for lo in (0, half):
-            for t in range(PACK):
-                quantize_w2(t, lo, lo + half)
+        nc.vector.tensor_copy(warm_plane[:].bitcast(I32).rearrange("p (r n) -> p r n", n=SEED // 4),
+                              seed_plane[:].bitcast(I32).unsqueeze(1).to_broadcast([P, S // SEED, SEED // 4]))
+        early = half + WARM_M
+        nc.vector.tensor_copy(w2_dst[:, half:early, :1], w2_src[:, half:early, :1])
+        nc.vector.tensor_copy(w2_dst[:, half:early, 1:], w2_src[:, half:early, 1:])
+        quantize_w2(0, half, early)
+        round_w2(early, P)
+        quantize_w2(0, early, P)
+        for t in range(1, PACK):
+            quantize_w2(t, half, P)
+        for t in range(PACK):
+            quantize_w2(t, 0, half)
 
         warm_bank = psum.tile([WARM_M, S], F32, name="warm_bank", tag="hidden3_0")
-        for i in range(WARM_PASSES):
-            nc.tensor.matmul_mx(out=warm_bank[:], lhsT=warm_codes[:, :WARM_M].bitcast(FP8X4), lhsT_scale=warm_plane[:, :WARM_M],
-                                rhs=warm_codes[:].bitcast(FP8X4), rhs_scale=warm_plane[:], start=True, stop=True)
+        for width in WARM_WIDTHS:
+            nc.tensor.matmul_mx(out=warm_bank[:, :width], lhsT=w2_codes[:, half:early].bitcast(FP8X4), lhsT_scale=w2_plane[:, half:early],
+                                rhs=warm_codes[:, :width].bitcast(FP8X4), rhs_scale=warm_plane[:, :width], start=True, stop=True)
 
         x_codes = []
         for g in range(S // GATHER):

@@ -19,7 +19,7 @@ PACK = 4
 GATHER = 256
 CHUNK = 128
 W2_SCALAR = 64
-W2_FIRST = 512
+W2_FIRST = 640
 WARM_WIDTHS = (512, 512, 128)
 SEED = 32
 WARM_M = 32

@@ -70,6 +70,8 @@ def tile_picked_phlora_gelu_p_kernel(tc, x_words, x_scales, w1, w2, w3, offs, ou
         warm_plane = keep.tile([P, S], U8, name="warm_plane", align_bytes=64)
         nc.vector.tensor_copy(warm_codes[:].bitcast(I32).rearrange("p (r n) -> p r n", n=SEED),
                               seed_codes[:].bitcast(I32).unsqueeze(1).to_broadcast([P, S // SEED, SEED]))
+        nc.scalar.copy(warm_plane[:].bitcast(U32).rearrange("p (r n) -> p r n", n=SEED // 4),
+                       seed_plane[:].bitcast(U32).unsqueeze(1).to_broadcast([P, S // SEED, SEED // 4]))
         w3_raw = shared.tile([P, PACK, N], F32, name="w3_raw", offset=T)
         nc.sync.dma_start(w3_raw[:], w3.rearrange("(p j) c -> p j c", j=PACK))
 
@@ -88,13 +90,11 @@ def tile_picked_phlora_gelu_p_kernel(tc, x_words, x_scales, w1, w2, w3, offs, ou
             cols = slice(t * P + lo, t * P + hi)
             nc.vector.quantize_mx(out=w2_codes[:, cols].bitcast(FP8X4), scales=w2_plane[:, cols], in_=w2_bf[:, t, lo:hi, :].rearrange("p m j -> p (m j)"))
 
-        nc.vector.tensor_copy(warm_plane[:].bitcast(I32).rearrange("p (r n) -> p r n", n=SEED // 4),
-                              seed_plane[:].bitcast(I32).unsqueeze(1).to_broadcast([P, S // SEED, SEED // 4]))
         early = half + WARM_M
         nc.vector.tensor_copy(w2_dst[:, half:early, :1], w2_src[:, half:early, :1])
-        nc.vector.tensor_copy(w2_dst[:, half:early, 1:], w2_src[:, half:early, 1:])
-        quantize_w2(0, half, early)
         round_w2(early, P)
+        quantize_w2(0, half, early)
+        nc.vector.tensor_copy(w2_dst[:, half:early, 1:], w2_src[:, half:early, 1:])
         quantize_w2(0, early, P)
         for t in range(1, PACK):
             quantize_w2(t, half, P)

@@ -19,7 +19,7 @@ PACK = 4
 GATHER = 256
 CHUNK = 128
 W2_SCALAR = 64
-W2_FIRST = 640
+W2_FIRST = 512
 WARM_WIDTHS = (512, 512, 128)
 SEED = 32
 WARM_M = 32
@@ -36,27 +36,27 @@ def tile_picked_phlora_gelu_p_kernel(tc, x_words, x_scales, w1, w2, w3, offs, ou
         shared = ctx.enter_context(tc.tile_pool(name="shared", bufs=1))
         psum = ctx.enter_context(tc.psum_pool(name="psum", bufs=1))
 
-        scale_table = shared.tile([P, T], U8, name="scale_table", offset=T // 2)
+        scale_table = shared.tile([P, T], U8, name="scale_table", offset=T // 2, align_bytes=256)
         nc.vector.memset(scale_table[:, : T // 2].bitcast(I32), 0)
         nc.gpsimd.memset(scale_table[:, T // 2 :].bitcast(I32), 0)
 
-        w2_raw = keep.tile([P, PACK * H], F32, name="w2_raw")
+        w2_raw = keep.tile([P, PACK * H], F32, name="w2_raw", align_bytes=256)
         w2_rows = w2.rearrange("(p j) c -> p (j c)", j=PACK)
         nc.sync.dma_start(w2_raw[:, :W2_FIRST], w2_rows[:, :W2_FIRST])
-        lists = keep.tile([P, S // 16], U16, name="lists")
+        lists = keep.tile([P, S // 16], U16, name="lists", align_bytes=256)
         nc.sync.dma_start(lists[:], offs)
         nc.sync.dma_start(scale_table[0:P:8, :].bitcast(I32), x_scales[0].bitcast(I32))
         nc.sync.dma_start(w2_raw[:, W2_FIRST:], w2_rows[:, W2_FIRST:])
-        word_table = keep.tile([P, T], U32, name="word_table", align_bytes=64)
+        word_table = keep.tile([P, T], U32, name="word_table", align_bytes=256)
         nc.sync.dma_start(word_table[:].bitcast(I32), x_words[0].rearrange("p n t -> p (n t)").bitcast(I32))
 
-        w1_raw = keep.tile([P, PACK, N], F32, name="w1_raw")
+        w1_raw = keep.tile([P, PACK, N], F32, name="w1_raw", align_bytes=256)
         nc.sync.dma_start(w1_raw[:], w1.rearrange("(p j) c -> p j c", j=PACK))
 
-        x_plane = keep.tile([P, S], U8, name="x_plane", align_bytes=64)
+        x_plane = keep.tile([P, S], U8, name="x_plane", align_bytes=256)
         nc.vector.memset(x_plane[:].bitcast(I32), 0)
 
-        picked_scales = keep.tile([P, S], U8, name="picked_scales", align_bytes=64)
+        picked_scales = keep.tile([P, S], U8, name="picked_scales", align_bytes=256)
         nc.vector.tensor_copy(picked_scales[:], scale_table[:].indirect(lists[:]))
         for r in range(4):
             nc.sync.dma_start(x_plane[r:P:32, :].bitcast(I32), picked_scales[8 * r : P : 32, :].bitcast(I32))
@@ -72,7 +72,7 @@ def tile_picked_phlora_gelu_p_kernel(tc, x_words, x_scales, w1, w2, w3, offs, ou
                               seed_codes[:].bitcast(I32).unsqueeze(1).to_broadcast([P, S // SEED, SEED]))
         nc.scalar.copy(warm_plane[:].bitcast(U32).rearrange("p (r n) -> p r n", n=SEED // 4),
                        seed_plane[:].bitcast(U32).unsqueeze(1).to_broadcast([P, S // SEED, SEED // 4]))
-        w3_raw = shared.tile([P, PACK, N], F32, name="w3_raw", offset=T)
+        w3_raw = shared.tile([P, PACK, N], F32, name="w3_raw", offset=T, align_bytes=256)
         nc.sync.dma_start(w3_raw[:], w3.rearrange("(p j) c -> p j c", j=PACK))
 
         w2_bf = keep.tile([P, PACK, P, PACK], BF16, name="w2_bf", align_bytes=64)
@@ -165,7 +165,7 @@ def tile_picked_phlora_gelu_p_kernel(tc, x_words, x_scales, w1, w2, w3, offs, ou
             nc.vector.quantize_mx(out=h_codes[:, cols].bitcast(FP8X4), scales=h_plane[:, cols], in_=h_bf[:].rearrange("p n t -> p (n t)"))
 
         for lo, hi in STORES:
-            result = keep.tile([P, hi - lo], F32, name="result%d" % lo)
+            result = keep.tile([P, hi - lo], F32, name="result%d" % lo, align_bytes=256)
             for c in range(lo // CHUNK, hi // CHUNK):
                 codes, plane = x_operand(c)
                 cols = slice(c * CHUNK, (c + 1) * CHUNK)
@@ -178,7 +178,7 @@ def tile_picked_phlora_gelu_p_kernel(tc, x_words, x_scales, w1, w2, w3, offs, ou
                 nc.scalar.copy(part, acc[:])
             nc.sync.dma_start(out[:, lo:hi], result[:])
 
-        result = keep.tile([P, CHUNK], F32, name="result_last")
+        result = keep.tile([P, CHUNK], F32, name="result_last", align_bytes=256)
         for lo, tag in ((0, "hidden0_2"), (NARROW, "hidden1_0")):
             cols = slice(last + lo, last + lo + NARROW)
             acc = psum.tile([P, NARROW], F32, name="acc_last%d" % lo, tag=tag)

@@ -37,8 +37,7 @@ def tile_picked_phlora_gelu_p_kernel(tc, x_words, x_scales, w1, w2, w3, offs, ou
         psum = ctx.enter_context(tc.psum_pool(name="psum", bufs=1))
 
         scale_table = shared.tile([P, T], U8, name="scale_table", offset=T // 2, align_bytes=256)
-        nc.vector.memset(scale_table[:, : T // 2].bitcast(I32), 0)
-        nc.gpsimd.memset(scale_table[:, T // 2 :].bitcast(I32), 0)
+        nc.vector.memset(scale_table[:].bitcast(I32), 0)
 
         w2_raw = keep.tile([P, PACK * H], F32, name="w2_raw", align_bytes=256)
         w2_rows = w2.rearrange("(p j) c -> p (j c)", j=PACK)

@@ -133,7 +133,7 @@ def tile_picked_phlora_gelu_p_kernel(tc, x_words, x_scales, w1, w2, w3, offs, ou
         w13_bf = keep.tile([P, 2, N, PACK], BF16, name="w13_bf", align_bytes=64)
         w13_codes = keep.tile([P, 2, N], U32, name="w13_codes", align_bytes=64)
         w13_plane = keep.tile([P, 2, N], U8, name="w13_plane", align_bytes=64)
-        nc.scalar.copy(w13_bf[:, 0].rearrange("p (c i) j -> p c j i", i=4), w1_raw[:].rearrange("p j (c i) -> p c j i", i=4))
+        nc.vector.tensor_copy(w13_bf[:, 0].rearrange("p (c i) j -> p c j i", i=4), w1_raw[:].rearrange("p j (c i) -> p c j i", i=4))
         nc.vector.tensor_copy(w13_bf[:, 1].rearrange("p (c i) j -> p c j i", i=4), w3_raw[:].rearrange("p j (c i) -> p c j i", i=4))
         for w in range(2):
             nc.vector.quantize_mx(out=w13_codes[:, w].bitcast(FP8X4), scales=w13_plane[:, w], in_=w13_bf[:, w].rearrange("p c j -> p (c j)"))

@@ -135,16 +135,6 @@ def tile_picked_phlora_gelu_p_kernel(tc, x_words, x_scales, w1, w2, w3, offs, ou
         w13_plane = keep.tile([P, 2, N], U8, name="w13_plane", align_bytes=64)
         nc.vector.tensor_copy(w13_bf[:, 0].rearrange("p (c i) j -> p c j i", i=4), w1_raw[:].rearrange("p j (c i) -> p c j i", i=4))
         nc.vector.tensor_copy(w13_bf[:, 1].rearrange("p (c i) j -> p c j i", i=4), w3_raw[:].rearrange("p j (c i) -> p c j i", i=4))
-        for w in range(2):
-            nc.vector.quantize_mx(out=w13_codes[:, w].bitcast(FP8X4), scales=w13_plane[:, w], in_=w13_bf[:, w].rearrange("p c j -> p (c j)"))
-
-        last = S - CHUNK
-        codes, plane = x_operand(last // CHUNK)
-        base_bank = psum.tile([P, CHUNK], F32, name="base_bank")
-        nc.tensor.matmul_mx(out=base_bank[:], lhsT=w13_codes[:, 0].bitcast(FP8X4), lhsT_scale=w13_plane[:, 0],
-                            rhs=codes, rhs_scale=plane, start=True, stop=True)
-        base = keep.tile([P, CHUNK], F32, name="base")
-        nc.vector.tensor_copy(base[:], base_bank[:])
 
         h_codes = shared.tile([P, S], U32, name="h_codes", offset=T, align_bytes=64)
         h_plane = keep.tile([P, S], U8, name="h_plane", align_bytes=64)
@@ -155,6 +145,8 @@ def tile_picked_phlora_gelu_p_kernel(tc, x_words, x_scales, w1, w2, w3, offs, ou
                 nc.scalar.activation(pairs[:, u].rearrange("p (n t) -> p n t", t=2), hidden[c][u][:].rearrange("p t n -> p n t"), GELU)
             h_bf = keep.tile([P, CHUNK * PACK], BF16, name="h_woven%d" % c, align_bytes=64)
             nc.vector.tensor_copy(h_bf[:].bitcast(I32).rearrange("p (n u) -> p n u", u=2), pairs[:].bitcast(I32).rearrange("p u n -> p n u"))
+            nc.vector.quantize_mx(out=w13_codes[:].rearrange("p w c -> p (w c)").bitcast(FP8X4), scales=w13_plane[:].rearrange("p w c -> p (w c)"),
+                                  in_=w13_bf[:].rearrange("p w c j -> p (w c j)"))
             nc.vector.quantize_mx(out=h_codes[:, cols].bitcast(FP8X4), scales=h_plane[:, cols], in_=h_bf[:])
         for lo, hi in H_PIECES:
             cols = slice(lo, hi)
@@ -162,6 +154,14 @@ def tile_picked_phlora_gelu_p_kernel(tc, x_words, x_scales, w1, w2, w3, offs, ou
             h_bf = keep.tile([P, hi - lo, PACK], BF16, name="h_bf%d" % lo, align_bytes=64)
             nc.scalar.activation(h_bf[:], hidden[c][0][:, :, first : first + hi - lo].rearrange("p t n -> p n t"), GELU)
             nc.vector.quantize_mx(out=h_codes[:, cols].bitcast(FP8X4), scales=h_plane[:, cols], in_=h_bf[:].rearrange("p n t -> p (n t)"))
+
+        last = S - CHUNK
+        codes, plane = x_operand(last // CHUNK)
+        base_bank = psum.tile([P, CHUNK], F32, name="base_bank")
+        nc.tensor.matmul_mx(out=base_bank[:], lhsT=w13_codes[:, 0].bitcast(FP8X4), lhsT_scale=w13_plane[:, 0],
+                            rhs=codes, rhs_scale=plane, start=True, stop=True)
+        base = keep.tile([P, CHUNK], F32, name="base")
+        nc.vector.tensor_copy(base[:], base_bank[:])
 
         for lo, hi in STORES:
             result = keep.tile([P, hi - lo], F32, name="result%d" % lo, align_bytes=256)

from contextlib import ExitStack

import concourse.mybir as mybir

K, T, S, H, N = 512, 2048, 512, 512, 128
FLOPS = 2 * S * (K * H + K * N + H * N)

F32 = mybir.dt.float32
BF16 = mybir.dt.bfloat16
I32 = mybir.dt.int32
U32 = mybir.dt.uint32
U16 = mybir.dt.uint16
U8 = mybir.dt.uint8
FP8X4 = mybir.dt.float8_e4m3fn_x4
GELU = mybir.ActivationFunctionType.Gelu_apprx_tanh

P = 128
PACK = 4
GATHER = 256
CHUNK = 128
W2_SCALAR = 64
W2_FIRST = 512
WARM_WIDTHS = (512, 512, 128)
SEED = 32
WARM_M = 32
PAIRED = 1
H_PIECES = ((128, 256), (256, 384), (384, 448), (448, 512))
STORES = ((0, 128), (128, 256), (256, 384))
NARROW = 64


def tile_picked_phlora_gelu_p_kernel(tc, x_words, x_scales, w1, w2, w3, offs, out):
    nc = tc.nc
    with ExitStack() as ctx:
        keep = ctx.enter_context(tc.tile_pool(name="keep", bufs=1))
        shared = ctx.enter_context(tc.tile_pool(name="shared", bufs=1))
        psum = ctx.enter_context(tc.psum_pool(name="psum", bufs=1))

        scale_table = shared.tile([P, T], U8, name="scale_table", offset=T // 2, align_bytes=256)
        nc.vector.memset(scale_table[:].bitcast(I32), 0)

        w2_raw = keep.tile([P, PACK * H], F32, name="w2_raw", align_bytes=256)
        w2_rows = w2.rearrange("(p j) c -> p (j c)", j=PACK)
        nc.sync.dma_start(w2_raw[:, :W2_FIRST], w2_rows[:, :W2_FIRST])
        lists = keep.tile([P, S // 16], U16, name="lists", align_bytes=256)
        nc.sync.dma_start(lists[:], offs)
        nc.sync.dma_start(scale_table[0:P:8, :].bitcast(I32), x_scales[0].bitcast(I32))
        nc.sync.dma_start(w2_raw[:, W2_FIRST:], w2_rows[:, W2_FIRST:])
        word_table = keep.tile([P, T], U32, name="word_table", align_bytes=256)
        nc.sync.dma_start(word_table[:].bitcast(I32), x_words[0].rearrange("p n t -> p (n t)").bitcast(I32))

        w1_raw = keep.tile([P, PACK, N], F32, name="w1_raw", align_bytes=256)
        nc.sync.dma_start(w1_raw[:], w1.rearrange("(p j) c -> p j c", j=PACK))

        x_plane = keep.tile([P, S], U8, name="x_plane", align_bytes=256)
        nc.vector.memset(x_plane[:].bitcast(I32), 0)

        picked_scales = keep.tile([P, S], U8, name="picked_scales", align_bytes=256)
        nc.vector.tensor_copy(picked_scales[:], scale_table[:].indirect(lists[:]))
        for r in range(4):
            nc.sync.dma_start(x_plane[r:P:32, :].bitcast(I32), picked_scales[8 * r : P : 32, :].bitcast(I32))

        seed_bf = keep.tile([P, PACK * SEED], BF16, name="seed_bf", align_bytes=64)
        nc.scalar.activation(seed_bf[:], w2_raw[:, : PACK * SEED], GELU)
        seed_codes = keep.tile([P, SEED], U32, name="seed_codes", align_bytes=64)
        seed_plane = keep.tile([P, SEED], U8, name="seed_plane", align_bytes=64)
        nc.vector.quantize_mx(out=seed_codes[:].bitcast(FP8X4), scales=seed_plane[:], in_=seed_bf[:])
        warm_codes = keep.tile([P, S], U32, name="warm_codes", align_bytes=64)
        warm_plane = keep.tile([P, S], U8, name="warm_plane", align_bytes=64)
        nc.vector.tensor_copy(warm_codes[:].bitcast(I32).rearrange("p (r n) -> p r n", n=SEED),
                              seed_codes[:].bitcast(I32).unsqueeze(1).to_broadcast([P, S // SEED, SEED]))
        nc.scalar.copy(warm_plane[:].bitcast(U32).rearrange("p (r n) -> p r n", n=SEED // 4),
                       seed_plane[:].bitcast(U32).unsqueeze(1).to_broadcast([P, S // SEED, SEED // 4]))
        w3_raw = shared.tile([P, PACK, N], F32, name="w3_raw", offset=T, align_bytes=256)
        nc.sync.dma_start(w3_raw[:], w3.rearrange("(p j) c -> p j c", j=PACK))

        w2_bf = keep.tile([P, PACK, P, PACK], BF16, name="w2_bf", align_bytes=64)
        w2_dst = w2_bf[:].rearrange("p t m j -> p m t j")
        w2_src = w2_raw[:].rearrange("p (j m t) -> p m t j", j=PACK, t=PACK)
        nc.scalar.copy(w2_dst[:, :W2_SCALAR], w2_src[:, :W2_SCALAR])
        half = P // 2
        w2_codes = keep.tile([P, H], U32, name="w2_codes", align_bytes=64)
        w2_plane = keep.tile([P, H], U8, name="w2_plane", align_bytes=64)

        def round_w2(lo, hi):
            nc.vector.tensor_copy(w2_dst[:, lo:hi], w2_src[:, lo:hi])

        def quantize_w2(t, lo, hi):
            cols = slice(t * P + lo, t * P + hi)
            nc.vector.quantize_mx(out=w2_codes[:, cols].bitcast(FP8X4), scales=w2_plane[:, cols], in_=w2_bf[:, t, lo:hi, :].rearrange("p m j -> p (m j)"))

        early = half + WARM_M
        nc.vector.tensor_copy(w2_dst[:, half:early, :1], w2_src[:, half:early, :1])
        round_w2(early, P)
        quantize_w2(0, half, early)
        nc.vector.tensor_copy(w2_dst[:, half:early, 1:], w2_src[:, half:early, 1:])
        quantize_w2(0, early, P)
        for t in range(1, PACK):
            quantize_w2(t, half, P)
        for t in range(PACK):
            quantize_w2(t, 0, half)

        warm_bank = psum.tile([WARM_M, S], F32, name="warm_bank", tag="hidden3_0")
        for width in WARM_WIDTHS:
            nc.tensor.matmul_mx(out=warm_bank[:, :width], lhsT=w2_codes[:, half:early].bitcast(FP8X4), lhsT_scale=w2_plane[:, half:early],
                                rhs=warm_codes[:, :width].bitcast(FP8X4), rhs_scale=warm_plane[:, :width], start=True, stop=True)

        x_codes = []
        for g in range(S // GATHER):
            picked = keep.tile([P, GATHER], U32, name="x_codes%d" % g, align_bytes=64)
            cols = GATHER // 16
            nc.vector.tensor_copy(picked[:], word_table[:].indirect(lists[:, g * cols : (g + 1) * cols]))
            x_codes.append(picked)

        def x_operand(c):
            g, lo = divmod(c * CHUNK, GATHER)
            return x_codes[g][:, lo : lo + CHUNK].bitcast(FP8X4), x_plane[:, c * CHUNK : (c + 1) * CHUNK]

        hidden = []
        for c in range(S // CHUNK):
            codes, plane = x_operand(c)
            width = 2 if c < PAIRED else PACK
            banks = []
            for first in range(0, PACK, width):
                bank = psum.tile([P, width, CHUNK], F32, name="hidden%d_%d" % (c, first))
                for t in range(width):
                    cols = slice((first + t) * P, (first + t + 1) * P)
                    nc.tensor.matmul_mx(out=bank[:, t, :], lhsT=w2_codes[:, cols].bitcast(FP8X4), lhsT_scale=w2_plane[:, cols],
                                        rhs=codes, rhs_scale=plane, start=True, stop=True)
                banks.append(bank)
            hidden.append(banks)

        w13_bf = keep.tile([P, 2, N, PACK], BF16, name="w13_bf", align_bytes=64)
        w13_codes = keep.tile([P, 2, N], U32, name="w13_codes", align_bytes=64)
        w13_plane = keep.tile([P, 2, N], U8, name="w13_plane", align_bytes=64)
        nc.vector.tensor_copy(w13_bf[:, 0].rearrange("p (c i) j -> p c j i", i=4), w1_raw[:].rearrange("p j (c i) -> p c j i", i=4))
        nc.vector.tensor_copy(w13_bf[:, 1].rearrange("p (c i) j -> p c j i", i=4), w3_raw[:].rearrange("p j (c i) -> p c j i", i=4))

        h_codes = shared.tile([P, S], U32, name="h_codes", offset=T, align_bytes=64)
        h_plane = keep.tile([P, S], U8, name="h_plane", align_bytes=64)
        for c in range(PAIRED):
            cols = slice(c * CHUNK, (c + 1) * CHUNK)
            pairs = keep.tile([P, 2, CHUNK * 2], BF16, name="pairs%d" % c, align_bytes=64)
            for u in range(2):
                nc.scalar.activation(pairs[:, u].rearrange("p (n t) -> p n t", t=2), hidden[c][u][:].rearrange("p t n -> p n t"), GELU)
            h_bf = keep.tile([P, CHUNK * PACK], BF16, name="h_woven%d" % c, align_bytes=64)
            nc.vector.tensor_copy(h_bf[:].bitcast(I32).rearrange("p (n u) -> p n u", u=2), pairs[:].bitcast(I32).rearrange("p u n -> p n u"))
            nc.vector.quantize_mx(out=w13_codes[:].rearrange("p w c -> p (w c)").bitcast(FP8X4), scales=w13_plane[:].rearrange("p w c -> p (w c)"),
                                  in_=w13_bf[:].rearrange("p w c j -> p (w c j)"))
            nc.vector.quantize_mx(out=h_codes[:, cols].bitcast(FP8X4), scales=h_plane[:, cols], in_=h_bf[:])
        for lo, hi in H_PIECES:
            cols = slice(lo, hi)
            c, first = divmod(lo, CHUNK)
            h_bf = keep.tile([P, hi - lo, PACK], BF16, name="h_bf%d" % lo, align_bytes=64)
            nc.scalar.activation(h_bf[:], hidden[c][0][:, :, first : first + hi - lo].rearrange("p t n -> p n t"), GELU)
            nc.vector.quantize_mx(out=h_codes[:, cols].bitcast(FP8X4), scales=h_plane[:, cols], in_=h_bf[:].rearrange("p n t -> p (n t)"))

        last = S - CHUNK
        codes, plane = x_operand(last // CHUNK)
        base_bank = psum.tile([P, CHUNK], F32, name="base_bank")
        nc.tensor.matmul_mx(out=base_bank[:], lhsT=w13_codes[:, 0].bitcast(FP8X4), lhsT_scale=w13_plane[:, 0],
                            rhs=codes, rhs_scale=plane, start=True, stop=True)
        base = keep.tile([P, CHUNK], F32, name="base")
        nc.vector.tensor_copy(base[:], base_bank[:])

        for lo, hi in STORES:
            result = keep.tile([P, hi - lo], F32, name="result%d" % lo, align_bytes=256)
            for c in range(lo // CHUNK, hi // CHUNK):
                codes, plane = x_operand(c)
                cols = slice(c * CHUNK, (c + 1) * CHUNK)
                acc = psum.tile([P, CHUNK], F32, name="acc%d" % c, tag="hidden0_0" if c == 0 else "acc%d" % c)
                nc.tensor.matmul_mx(out=acc[:], lhsT=w13_codes[:, 0].bitcast(FP8X4), lhsT_scale=w13_plane[:, 0],
                                    rhs=codes, rhs_scale=plane, start=True, stop=False)
                nc.tensor.matmul_mx(out=acc[:], lhsT=w13_codes[:, 1].bitcast(FP8X4), lhsT_scale=w13_plane[:, 1],
                                    rhs=h_codes[:, cols].bitcast(FP8X4), rhs_scale=h_plane[:, cols], start=False, stop=True)
                part = result[:, c * CHUNK - lo : (c + 1) * CHUNK - lo]
                nc.scalar.copy(part, acc[:])
            nc.sync.dma_start(out[:, lo:hi], result[:])

        result = keep.tile([P, CHUNK], F32, name="result_last", align_bytes=256)
        for lo, tag in ((0, "hidden0_2"), (NARROW, "hidden1_0")):
            cols = slice(last + lo, last + lo + NARROW)
            acc = psum.tile([P, NARROW], F32, name="acc_last%d" % lo, tag=tag)
            nc.tensor.matmul_mx(out=acc[:], lhsT=w13_codes[:, 1].bitcast(FP8X4), lhsT_scale=w13_plane[:, 1],
                                rhs=h_codes[:, cols].bitcast(FP8X4), rhs_scale=h_plane[:, cols], start=True, stop=True)
            nc.vector.tensor_tensor(result[:, lo : lo + NARROW], acc[:], base[:, lo : lo + NARROW], mybir.AluOpType.add)
        nc.sync.dma_start(out[:, last:], result[:])
